import numpy as np
import ml_dtypes


def mxq(x, axis, fmt="e4m3"):
    dtype, down = {"e4m3": (ml_dtypes.float8_e4m3fn, 7), "e5m2": (ml_dtypes.float8_e5m2, 14)}[fmt]
    v = np.moveaxis(np.asarray(x, np.float32).astype(ml_dtypes.bfloat16).astype(np.float64), axis, -1)
    blocks = v.reshape(v.shape[:-1] + (-1, 32))
    amax = np.abs(blocks).max(-1, keepdims=True)
    byte = np.maximum(np.where(amax > 0, np.frexp(amax)[1] - 1 + 127, 0) - down, 1)
    scale = np.exp2(byte - 127.0)
    codes = (blocks / scale).astype(np.float32).astype(dtype).astype(np.float64)
    return np.moveaxis((codes * scale).reshape(v.shape), -1, axis)


WIDE = False


def mx_kscale(k):
    if not WIDE:
        return np.ones(k)
    levels = np.array([10, -10, 5, -5, 0])
    if k % 512:
        return np.exp2(np.random.permutation(np.resize(levels, k // 32))).repeat(32)
    a = np.empty((k // 512, 16))
    for p in range(k // 512):
        a[p, :8] = np.random.permutation(np.resize(levels, 8))
        for g in range(8):
            far = levels[np.abs(levels - a[p, g]) >= 10]
            a[p, g + 8] = far[np.random.randint(len(far))]
    return np.exp2(a.ravel()).repeat(32)


def f64(x):
    return np.asarray(x).astype(np.float64)


def striped(idx):
    return np.tile(idx.reshape(-1, 16).T, (8, 1)).astype(np.uint16)


def unstriped(offs):
    return offs[:16].T.reshape(-1).astype(np.int64)


E2M1 = np.array([0.0, 0.5, 1.0, 1.5, 2.0, 3.0, 4.0, 6.0, -0.0, -0.5, -1.0, -1.5, -2.0, -3.0, -4.0, -6.0])


def pack_weight(w, fmt):
    k, n = w.shape
    w = f64(np.asarray(w, np.float32).astype(ml_dtypes.bfloat16)).reshape(k // 32, 32, n)
    amax = np.abs(w).max(1)
    if fmt == "e4m3":
        byte = np.frexp(amax)[1] - 1 + 127 - 7
    else:
        mant, ex = np.frexp(amax / 6.0)
        byte = np.where(mant > 0.5, ex, ex - 1) + 127
    byte = np.clip(np.where(amax > 0, byte, 1), 1, 254)
    scaled = (w * np.exp2(127.0 - byte)[:, None, :]).reshape(k, n).astype(np.float32)
    by_word = np.ascontiguousarray(scaled.reshape(k // 512, 128, 4, n).transpose(0, 1, 3, 2))
    if fmt == "e4m3":
        words = by_word.astype(ml_dtypes.float8_e4m3fn).view(np.uint8)
    else:
        c = by_word.astype(ml_dtypes.float4_e2m1fn).view(np.uint8) & 0xF
        words = (c[..., 0::2] | (c[..., 1::2] << 4)).reshape(k // 512, 128, 2 * n)
    return np.ascontiguousarray(words), np.ascontiguousarray(byte.astype(np.uint8).reshape(k // 512, 16, n))


def unpack_weight(words, scales, fmt):
    g, _, n = scales.shape
    words = np.ascontiguousarray(words).reshape(g, 128, n, -1)
    if fmt == "e4m3":
        vals = words.view(ml_dtypes.float8_e4m3fn).astype(np.float64)
    else:
        nib = np.empty((g, 128, n, 4), np.uint8)
        nib[..., 0::2] = words & 0xF
        nib[..., 1::2] = words >> 4
        vals = E2M1[nib]
    vals = vals * np.repeat(np.exp2(scales.astype(np.float64) - 127.0), 8, axis=1)[..., None]
    return vals.transpose(0, 1, 3, 2).reshape(g * 512, n)


def pack_table(v):
    words, scales = pack_weight(v, "e4m3")
    return np.concatenate([words.reshape(words.shape[0], -1), scales.reshape(scales.shape[0], -1)], axis=1)


def unpack_table(tab):
    g, t = tab.shape[0], tab.shape[1] // 528
    return unpack_weight(tab[:, :512 * t].reshape(g, 128, t, 4), tab[:, 512 * t:].reshape(g, 16, t), "e4m3")


def silu(v):
    return v / (1.0 + np.exp(-np.maximum(v, -700.0)))


O, K, M, T, S = 1024, 1536, 1024, 4096, 1536


def setup_inputs():
    n = np.random.standard_normal
    s = mx_kscale(K)[:, None]
    w = n((K, M)) / np.sqrt(K) / s
    p_w4 = pack_weight(w[O:], "e2m1")
    return {
        "tab": pack_table(n((K, T)) * s),
        "w8": (w[:O]).astype(np.float32),
        "w4_words": p_w4[0],
        "w4_scales": p_w4[1],
        "b": (0.3 * n(1024)).astype(np.float32),
        "offs": striped(np.random.permutation(T)[:S]),
    }


def reference(tab, w8, w4_words, w4_scales, b, offs):
    tab_ = unpack_table(tab)[:, unstriped(offs)]
    w8_ = mxq(f64(w8), 0, "e4m3")
    w4_ = unpack_weight(w4_words, w4_scales, "e2m1")
    y = tab_[:O].T @ w8_ + tab_[O:].T @ w4_
    return silu(y + f64(b)[None, :])

@@ -1,0 +1,199 @@
+from contextlib import ExitStack
+
+import concourse.mybir as mybir
+from concourse.masks import make_identity
+
+F32 = mybir.dt.float32
+BF16 = mybir.dt.bfloat16
+I32 = mybir.dt.int32
+U32 = mybir.dt.uint32
+U16 = mybir.dt.uint16
+U8 = mybir.dt.uint8
+FP8X4 = mybir.dt.float8_e4m3fn_x4
+FP4X4 = mybir.dt.float4_e2m1fn_x4
+ADD = mybir.AluOpType.add
+MULT = mybir.AluOpType.mult
+SILU = mybir.ActivationFunctionType.Silu
+
+P = 128
+O, K, M, T, S = 1024, 1536, 1024, 4096, 1536
+FLOPS = 2 * K * M * S
+NH = 512
+PLANE = (4, 8, 0)
+TILES = S // P
+AHEAD = 8
+
+
+def tile_list_tabo_tm_silu_kernel(tc, tab, w8, w4_words, w4_scales, b, offs, out):
+    nc = tc.nc
+    with ExitStack() as ctx:
+        keep = ctx.enter_context(tc.tile_pool(name="keep", bufs=1))
+        zpool = ctx.enter_context(tc.tile_pool(name="zpool", bufs=6))
+        ypool = ctx.enter_context(tc.tile_pool(name="ypool", bufs=6))
+        psum = ctx.enter_context(tc.psum_pool(name="psum", bufs=8))
+
+        offsets = keep.tile([P, S // 16], U16, name="offsets")
+        words = [keep.tile([P, T], I32, name=f"words{a}", align_bytes=64) for a in range(3)]
+        planes = keep.tile([P, T], U8, name="planes", align_bytes=64)
+        gwords = [keep.tile([P, S], U32, name=f"gwords{a}", align_bytes=64) for a in range(3)]
+        gplanes = keep.tile([P, S], U8, name="gplanes", align_bytes=64)
+        raw = {}
+        grouped = {}
+        codes = {}
+        wscale = {}
+        for h in range(2):
+            for a in range(2):
+                raw[h, a] = keep.tile([P, 4, NH], F32, name=f"raw{h}{a}", align_bytes=64)
+                grouped[h, a] = keep.tile([P, NH, 4], BF16, name=f"grouped{h}{a}", align_bytes=64)
+                codes[h, a] = keep.tile([P, NH], U32, name=f"codes{h}{a}", align_bytes=64)
+                wscale[h, a] = keep.tile([P, NH], U8, name=f"wscale{h}{a}", align_bytes=64)
+        w4w = keep.tile([P, 2 * M], U8, name="w4w", align_bytes=64)
+        w4s = keep.tile([P, M], U8, name="w4s", align_bytes=64)
+        brows = keep.tile([P, P], F32, name="brows")
+        bcol = keep.tile([P, P], F32, name="bcol")
+        bias = keep.tile([P, M], F32, name="bias")
+        ident = keep.tile([P, P], F32, name="ident")
+        warm = keep.tile([P, 1], F32, name="warm")
+
+        nc.vector.memset(planes[:].bitcast(I32), 0)
+        nc.vector.memset(brows[:], 0.0)
+        nc.vector.memset(w4s[:].bitcast(I32), 0)
+        for a in (1, 2):
+            nc.vector.memset(words[a][:, 0:8], 0)
+        nc.vector.memset(w4w[:, 0:32].bitcast(I32), 0)
+        for h, a in ((0, 1), (1, 0), (1, 1)):
+            nc.vector.memset(raw[h, a][:, 0, 0:8], 0.0)
+        nc.vector.memset(warm[:], 0.0)
+        nc.scalar.activation(warm[:], warm[:], SILU)
+
+        def load_w8(h, a):
+            src = w8[512 * a : 512 * (a + 1), NH * h : NH * (h + 1)]
+            nc.sync.dma_start(out=raw[h, a][:], in_=src.rearrange("(p j) w -> p j w", j=4))
+
+        def load_words(a):
+            src = tab[a, 0 : 512 * T].rearrange("(p x) -> p x", p=P)
+            nc.sync.dma_start(out=words[a][:], in_=src.bitcast(I32))
+
+        nc.sync.dma_start(offsets[:], offs)
+        load_words(0)
+        load_w8(0, 0)
+        for q in range(4):
+            src = tab[0:2, (512 + 4 * q) * T : (516 + 4 * q) * T].rearrange("a (r t) -> a r t", r=4)
+            k = 32 * q + PLANE[0]
+            nc.gpsimd.dma_start(out=planes[k : k + 8, :].bitcast(I32), in_=src.bitcast(I32))
+        for q in range(4):
+            src = tab[2, (512 + 4 * q) * T : (516 + 4 * q) * T].rearrange("(r t) -> r t", r=4)
+            k = 32 * q + PLANE[2]
+            nc.sync.dma_start(out=planes[k : k + 4, :].bitcast(I32), in_=src.bitcast(I32))
+        load_w8(0, 1)
+        nc.sync.dma_start(out=brows[0:8, :], in_=b.rearrange("(c p) -> c p", p=P))
+        load_words(1)
+        nc.sync.dma_start(out=w4w[:].bitcast(I32), in_=w4_words[0].bitcast(I32))
+        for q in range(4):
+            nc.sync.dma_start(
+                out=w4s[32 * q : 32 * q + 4, :].bitcast(I32), in_=w4_scales[0, 4 * q : 4 * q + 4, :].bitcast(I32)
+            )
+        load_words(2)
+        load_w8(1, 0)
+        load_w8(1, 1)
+
+        make_identity(nc, ident[:])
+
+        def interleave(engine, h, a, lo, hi):
+            src = raw[h, a][:, :, lo:hi].rearrange("p j w -> p w j")
+            dst = grouped[h, a][:, lo:hi, :]
+            if engine == "scalar":
+                nc.scalar.copy(dst, src)
+            elif engine == "vector":
+                nc.vector.tensor_copy(dst, src)
+            else:
+                nc.gpsimd.tensor_scalar(dst, src, 1.0, 0.0, MULT, ADD)
+
+        def quantize(h, a):
+            nc.vector.quantize_mx(
+                out=codes[h, a][:].bitcast(FP8X4),
+                scales=wscale[h, a][:],
+                in_=grouped[h, a][:].rearrange("p w j -> p (w j)"),
+            )
+
+        interleave("scalar", 0, 0, 0, NH)
+        interleave("scalar", 0, 1, 0, NH)
+
+        pt = psum.tile([P, NH], F32, name="acc")
+        nc.tensor.transpose(pt[:, 0:P], brows[:], ident[:])
+        nc.scalar.copy(bcol[:], pt[:, 0:P])
+        for h in range(2):
+            pb = psum.tile([P, NH], F32, name="acc")
+            for c in range(4):
+                col = bcol[:, 4 * h + c : 4 * h + c + 1].to_broadcast([P, P])
+                nc.tensor.transpose(pb[:, c * P : (c + 1) * P], col, ident[:])
+            nc.scalar.copy(bias[:, NH * h : NH * (h + 1)], pb[:])
+
+        def gather_words(a, lo, hi):
+            nc.vector.tensor_copy(
+                gwords[a][:, lo:hi], words[a][:].bitcast(U32).indirect(offsets[:, lo // 16 : hi // 16])
+            )
+
+
+        def mm(acc, t, h, a):
+            cols = slice(t * P, (t + 1) * P)
+            if a < 2:
+                rhs = codes[h, a][:].bitcast(FP8X4)
+                rhs_scale = wscale[h, a][:]
+            else:
+                rhs = w4w[:, 2 * NH * h : 2 * NH * (h + 1)].bitcast(FP4X4)
+                rhs_scale = w4s[:, NH * h : NH * (h + 1)]
+            nc.tensor.matmul_mx(
+                out=acc[:],
+                lhsT=gwords[a][:, cols].bitcast(FP8X4),
+                lhsT_scale=gplanes[PLANE[a] : P, cols],
+                rhs=rhs,
+                rhs_scale=rhs_scale,
+                start=(a == 0),
+                stop=(a == 2),
+            )
+
+        ybuf = {}
+
+        def epilogue(acc, t, h):
+            z = zpool.tile([P, NH], F32, name="z")
+            nc.vector.tensor_tensor(out=z[:], in0=acc[:], in1=bias[:, NH * h : NH * (h + 1)], op=ADD)
+            paired = (t, h) not in ((0, 0), (1, 0), (TILES - 2, 1), (TILES - 1, 1))
+            n = 2 if paired else 1
+            u = t % 2 if paired else 0
+            if u == 0:
+                ybuf[n] = ypool.tile([P, n, NH], F32, name=f"y{n}")
+            y = ybuf[n]
+            nc.scalar.activation(y[:, u, :], z[:], SILU)
+            if u == n - 1:
+                dst = out[(t - u) * P : (t + 1) * P, NH * h : NH * (h + 1)]
+                nc.sync.dma_start(out=dst.rearrange("(u p) w -> p u w", p=P), in_=y[:])
+
+        accs = []
+        for t in range(AHEAD):
+            accs.append(psum.tile([P, NH], F32, name="acc"))
+        gather_words(0, 0, S)
+        nc.vector.tensor_copy(gplanes[:], planes[:].indirect(offsets[:]))
+        quantize(0, 0)
+        quantize(0, 1)
+        for t in range(AHEAD):
+            mm(accs[t], t, 0, 0)
+        gather_words(1, 0, S)
+        for t in range(AHEAD):
+            mm(accs[t], t, 0, 1)
+        for t in range(AHEAD):
+            if t % 4 == 0:
+                gather_words(2, t * P, t * P + 512)
+            mm(accs[t], t, 0, 2)
+            epilogue(accs[t], t, 0)
+        gather_words(2, AHEAD * P, S)
+        for a in range(2):
+            for lo in (0, NH // 2):
+                interleave("gpsimd", 1, a, lo, lo + NH // 2)
+            quantize(1, a)
+        order = [(t, 0) for t in range(AHEAD, TILES)] + [(t, 1) for t in range(TILES)]
+        for t, h in order:
+            acc = psum.tile([P, NH], F32, name="acc")
+            for a in range(3):
+                mm(acc, t, h, a)
+            epilogue(acc, t, h)

@@ -22,178 +22,181 @@ NH = 512
 PLANE = (4, 8, 0)
 TILES = S // P
 AHEAD = 8
+NQ = NH // 2
 
 
 def tile_list_tabo_tm_silu_kernel(tc, tab, w8, w4_words, w4_scales, b, offs, out):
     nc = tc.nc
     with ExitStack() as ctx:
         keep = ctx.enter_context(tc.tile_pool(name="keep", bufs=1))
+        stage = ctx.enter_context(tc.tile_pool(name="stage", bufs=1))
         zpool = ctx.enter_context(tc.tile_pool(name="zpool", bufs=6))
-        ypool = ctx.enter_context(tc.tile_pool(name="ypool", bufs=6))
+        ypool = ctx.enter_context(tc.tile_pool(name="ypool", bufs=8))
         psum = ctx.enter_context(tc.psum_pool(name="psum", bufs=8))
 
+        def slot(tag, shape, dtype, name):
+            return keep.tile(shape, dtype, name=name, tag=tag, align_bytes=64)
+
+        def placed(offset, shape, dtype, name):
+            return stage.tile(shape, dtype, name=name, align_bytes=64, offset=offset)
+
         offsets = keep.tile([P, S // 16], U16, name="offsets")
-        words = [keep.tile([P, T], I32, name=f"words{a}", align_bytes=64) for a in range(3)]
-        planes = keep.tile([P, T], U8, name="planes", align_bytes=64)
-        gwords = [keep.tile([P, S], U32, name=f"gwords{a}", align_bytes=64) for a in range(3)]
+        gwords = {a: keep.tile([P, S], U32, name=f"gwords{a}", align_bytes=64) for a in (0, 2)}
+        gwords[1] = keep.tile([P, AHEAD * P], U32, name="gwords1", align_bytes=64)
         gplanes = keep.tile([P, S], U8, name="gplanes", align_bytes=64)
-        raw = {}
-        grouped = {}
         codes = {}
         wscale = {}
         for h in range(2):
             for a in range(2):
-                raw[h, a] = keep.tile([P, 4, NH], F32, name=f"raw{h}{a}", align_bytes=64)
-                grouped[h, a] = keep.tile([P, NH, 4], BF16, name=f"grouped{h}{a}", align_bytes=64)
                 codes[h, a] = keep.tile([P, NH], U32, name=f"codes{h}{a}", align_bytes=64)
                 wscale[h, a] = keep.tile([P, NH], U8, name=f"wscale{h}{a}", align_bytes=64)
         w4w = keep.tile([P, 2 * M], U8, name="w4w", align_bytes=64)
-        w4s = keep.tile([P, M], U8, name="w4s", align_bytes=64)
-        brows = keep.tile([P, P], F32, name="brows")
-        bcol = keep.tile([P, P], F32, name="bcol")
         bias = keep.tile([P, M], F32, name="bias")
-        ident = keep.tile([P, P], F32, name="ident")
         warm = keep.tile([P, 1], F32, name="warm")
+        planes = keep.tile([P, T], U8, name="planes", align_bytes=64)
+        bvec = slot("slot_a", [P, 8], F32, "bvec")
+        ident = placed(4 * T - 256, [P, P], F32, "ident")
 
         nc.vector.memset(planes[:].bitcast(I32), 0)
-        nc.vector.memset(brows[:], 0.0)
-        nc.vector.memset(w4s[:].bitcast(I32), 0)
-        for a in (1, 2):
-            nc.vector.memset(words[a][:, 0:8], 0)
-        nc.vector.memset(w4w[:, 0:32].bitcast(I32), 0)
-        for h, a in ((0, 1), (1, 0), (1, 1)):
-            nc.vector.memset(raw[h, a][:, 0, 0:8], 0.0)
         nc.vector.memset(warm[:], 0.0)
         nc.scalar.activation(warm[:], warm[:], SILU)
 
-        def load_w8(h, a):
-            src = w8[512 * a : 512 * (a + 1), NH * h : NH * (h + 1)]
-            nc.sync.dma_start(out=raw[h, a][:], in_=src.rearrange("(p j) w -> p j w", j=4))
+        def load_w8(dst, a, lo, hi):
+            src = w8[512 * a : 512 * (a + 1), lo:hi]
+            nc.sync.dma_start(out=dst, in_=src.rearrange("(p j) w -> p j w", j=4))
 
-        def load_words(a):
+        def load_words(words, a):
             src = tab[a, 0 : 512 * T].rearrange("(p x) -> p x", p=P)
-            nc.sync.dma_start(out=words[a][:], in_=src.bitcast(I32))
+            nc.sync.dma_start(out=words[:], in_=src.bitcast(I32))
 
         nc.sync.dma_start(offsets[:], offs)
-        load_words(0)
-        load_w8(0, 0)
-        for q in range(4):
+        nc.sync.dma_start(out=bvec[:], in_=b.rearrange("(p c) -> p c", c=8))
+        nc.sync.dma_start(out=w4w[:].bitcast(I32), in_=w4_words[0].bitcast(I32))
+        words0 = slot("slot_words", [P, T], I32, "words0")
+        load_words(words0, 0)
+        for q in range(3):
             src = tab[0:2, (512 + 4 * q) * T : (516 + 4 * q) * T].rearrange("a (r t) -> a r t", r=4)
             k = 32 * q + PLANE[0]
             nc.gpsimd.dma_start(out=planes[k : k + 8, :].bitcast(I32), in_=src.bitcast(I32))
-        for q in range(4):
-            src = tab[2, (512 + 4 * q) * T : (516 + 4 * q) * T].rearrange("(r t) -> r t", r=4)
-            k = 32 * q + PLANE[2]
+        for a, q in ((0, 3), (1, 3), (2, 0), (2, 1), (2, 2), (2, 3)):
+            src = tab[a, (512 + 4 * q) * T : (516 + 4 * q) * T].rearrange("(r t) -> r t", r=4)
+            k = 32 * q + PLANE[a]
             nc.sync.dma_start(out=planes[k : k + 4, :].bitcast(I32), in_=src.bitcast(I32))
-        load_w8(0, 1)
-        nc.sync.dma_start(out=brows[0:8, :], in_=b.rearrange("(c p) -> c p", p=P))
-        load_words(1)
-        nc.sync.dma_start(out=w4w[:].bitcast(I32), in_=w4_words[0].bitcast(I32))
+
+        make_identity(nc, ident[:])
+        for u in range(2):
+            pb = psum.tile([P, 4, P], F32, name="pb", tag="acc")
+            for c in range(4):
+                col = bvec[:, 4 * u + c : 4 * u + c + 1].to_broadcast([P, P])
+                nc.tensor.transpose(pb[:, c, :], col, ident[:])
+            dst = bias[:].rearrange("q (p c) -> q p c", c=8)[:, :, 4 * u : 4 * u + 4]
+            nc.scalar.copy(dst, pb[:].rearrange("q c p -> q p c"))
+
+        raw00 = slot("slot_a", [P, 4, NH], F32, "raw00")
+        load_w8(raw00[:], 0, 0, NH)
+        words2 = placed(0, [P, T], I32, "words2")
+        load_words(words2, 2)
+        w4s = placed(4 * T, [P, M], U8, "w4s")
+        nc.vector.memset(w4s[:].bitcast(I32), 0)
         for q in range(4):
             nc.sync.dma_start(
                 out=w4s[32 * q : 32 * q + 4, :].bitcast(I32), in_=w4_scales[0, 4 * q : 4 * q + 4, :].bitcast(I32)
             )
-        load_words(2)
-        load_w8(1, 0)
-        load_w8(1, 1)
 
-        make_identity(nc, ident[:])
-
-        def interleave(engine, h, a, lo, hi):
-            src = raw[h, a][:, :, lo:hi].rearrange("p j w -> p w j")
-            dst = grouped[h, a][:, lo:hi, :]
+        def interleave(engine, dst, src):
+            src = src.rearrange("p j w -> p w j")
             if engine == "scalar":
                 nc.scalar.copy(dst, src)
-            elif engine == "vector":
-                nc.vector.tensor_copy(dst, src)
             else:
                 nc.gpsimd.tensor_scalar(dst, src, 1.0, 0.0, MULT, ADD)
 
-        def quantize(h, a):
+        def quantize(h, a, grouped, lo, hi):
             nc.vector.quantize_mx(
-                out=codes[h, a][:].bitcast(FP8X4),
-                scales=wscale[h, a][:],
-                in_=grouped[h, a][:].rearrange("p w j -> p (w j)"),
+                out=codes[h, a][:, lo:hi].bitcast(FP8X4),
+                scales=wscale[h, a][:, lo:hi],
+                in_=grouped.rearrange("p w j -> p (w j)"),
             )
 
-        interleave("scalar", 0, 0, 0, NH)
-        interleave("scalar", 0, 1, 0, NH)
+        def gather_words(dst, words, lo, hi):
+            nc.vector.tensor_copy(dst, words[:].bitcast(U32).indirect(offsets[:, lo // 16 : hi // 16]))
 
-        pt = psum.tile([P, NH], F32, name="acc")
-        nc.tensor.transpose(pt[:, 0:P], brows[:], ident[:])
-        nc.scalar.copy(bcol[:], pt[:, 0:P])
-        for h in range(2):
-            pb = psum.tile([P, NH], F32, name="acc")
-            for c in range(4):
-                col = bcol[:, 4 * h + c : 4 * h + c + 1].to_broadcast([P, P])
-                nc.tensor.transpose(pb[:, c * P : (c + 1) * P], col, ident[:])
-            nc.scalar.copy(bias[:, NH * h : NH * (h + 1)], pb[:])
-
-        def gather_words(a, lo, hi):
-            nc.vector.tensor_copy(
-                gwords[a][:, lo:hi], words[a][:].bitcast(U32).indirect(offsets[:, lo // 16 : hi // 16])
-            )
-
-
-        def mm(acc, t, h, a):
+        def mm(acc, t, h, a, start, stop, lo=0, hi=NH):
             cols = slice(t * P, (t + 1) * P)
             if a < 2:
-                rhs = codes[h, a][:].bitcast(FP8X4)
-                rhs_scale = wscale[h, a][:]
+                rhs = codes[h, a][:, lo:hi].bitcast(FP8X4)
+                rhs_scale = wscale[h, a][:, lo:hi]
             else:
                 rhs = w4w[:, 2 * NH * h : 2 * NH * (h + 1)].bitcast(FP4X4)
                 rhs_scale = w4s[:, NH * h : NH * (h + 1)]
+            if a == 1 and t >= AHEAD:
+                lhsT = gwords["late"][:, (t - AHEAD) * P : (t - AHEAD + 1) * P]
+            else:
+                lhsT = gwords[a][:, cols]
             nc.tensor.matmul_mx(
-                out=acc[:],
-                lhsT=gwords[a][:, cols].bitcast(FP8X4),
+                out=acc[:, lo:hi],
+                lhsT=lhsT.bitcast(FP8X4),
                 lhsT_scale=gplanes[PLANE[a] : P, cols],
                 rhs=rhs,
                 rhs_scale=rhs_scale,
-                start=(a == 0),
-                stop=(a == 2),
+                start=start,
+                stop=stop,
             )
-
-        ybuf = {}
 
         def epilogue(acc, t, h):
             z = zpool.tile([P, NH], F32, name="z")
             nc.vector.tensor_tensor(out=z[:], in0=acc[:], in1=bias[:, NH * h : NH * (h + 1)], op=ADD)
-            paired = (t, h) not in ((0, 0), (1, 0), (TILES - 2, 1), (TILES - 1, 1))
-            n = 2 if paired else 1
-            u = t % 2 if paired else 0
-            if u == 0:
-                ybuf[n] = ypool.tile([P, n, NH], F32, name=f"y{n}")
-            y = ybuf[n]
-            nc.scalar.activation(y[:, u, :], z[:], SILU)
-            if u == n - 1:
-                dst = out[(t - u) * P : (t + 1) * P, NH * h : NH * (h + 1)]
-                nc.sync.dma_start(out=dst.rearrange("(u p) w -> p u w", p=P), in_=y[:])
+            y = ypool.tile([P, NH], F32, name="y")
+            nc.scalar.activation(y[:], z[:], SILU)
+            nc.sync.dma_start(out=out[t * P : (t + 1) * P, NH * h : NH * (h + 1)], in_=y[:])
 
-        accs = []
-        for t in range(AHEAD):
-            accs.append(psum.tile([P, NH], F32, name="acc"))
-        gather_words(0, 0, S)
+        gather_words(gwords[0][:], words0, 0, S)
+        words1 = slot("slot_words", [P, T], I32, "words1")
+        load_words(words1, 1)
         nc.vector.tensor_copy(gplanes[:], planes[:].indirect(offsets[:]))
-        quantize(0, 0)
-        quantize(0, 1)
+        grouped00 = keep.tile([P, NH, 4], BF16, name="grouped00", align_bytes=64)
+        interleave("scalar", grouped00[:], raw00[:])
+        quantize(0, 0, grouped00[:], 0, NH)
+        raw01 = slot("slot_a", [P, 2, 4, NQ], F32, "raw01")
+        for u in range(2):
+            load_w8(raw01[:, u], 1, u * NQ, (u + 1) * NQ)
+
+        accs = [psum.tile([P, NH], F32, name=f"acc{t}", tag="acc") for t in range(AHEAD)]
         for t in range(AHEAD):
-            mm(accs[t], t, 0, 0)
-        gather_words(1, 0, S)
-        for t in range(AHEAD):
-            mm(accs[t], t, 0, 1)
-        for t in range(AHEAD):
-            if t % 4 == 0:
-                gather_words(2, t * P, t * P + 512)
-            mm(accs[t], t, 0, 2)
-            epilogue(accs[t], t, 0)
-        gather_words(2, AHEAD * P, S)
+            mm(accs[t], t, 0, 0, True, False)
+        for lo in range(0, S, 512):
+            gather_words(gwords[2][:, lo : lo + 512], words2, lo, lo + 512)
+        raw1 = placed(0, [P, 2, 4, NH], F32, "raw1")
         for a in range(2):
-            for lo in (0, NH // 2):
-                interleave("gpsimd", 1, a, lo, lo + NH // 2)
-            quantize(1, a)
-        order = [(t, 0) for t in range(AHEAD, TILES)] + [(t, 1) for t in range(TILES)]
-        for t, h in order:
-            acc = psum.tile([P, NH], F32, name="acc")
+            load_w8(raw1[:, a], a, NH, M)
+        for t in range(AHEAD):
+            mm(accs[t], t, 0, 2, False, False)
+        for lo in range(0, AHEAD * P, 512):
+            gather_words(gwords[1][:, lo : lo + 512], words1, lo, lo + 512)
+        quarter0 = slot("slot_q", [P, NQ, 4], BF16, "quarter0")
+        interleave("scalar", quarter0[:], raw01[:, 0])
+        quantize(0, 1, quarter0[:], 0, NQ)
+        gwords["late"] = slot("slot_q", [P, S - AHEAD * P], U32, "gwords1late")
+        gather_words(gwords["late"][:], words1, AHEAD * P, S)
+        quarter1 = keep.tile([P, NQ, 4], BF16, name="quarter1", align_bytes=64)
+        interleave("scalar", quarter1[:], raw01[:, 1])
+        quantize(0, 1, quarter1[:], NQ, NH)
+        for a in range(2):
+            grouped = keep.tile([P, NH, 4], BF16, name=f"grouped1{a}", align_bytes=64)
+            for lo in range(0, NH, 128):
+                interleave("gpsimd", grouped[:, lo : lo + 128, :], raw1[:, a, :, lo : lo + 128])
+            quantize(1, a, grouped[:], 0, NH)
+        for t in range(AHEAD):
+            mm(accs[t], t, 0, 1, False, False, 0, NQ)
+        for t in range(AHEAD):
+            mm(accs[t], t, 0, 1, False, True, NQ, NH)
+            epilogue(accs[t], t, 0)
+        for t in range(AHEAD, TILES):
+            acc = psum.tile([P, NH], F32, name="acc", tag="acc")
             for a in range(3):
-                mm(acc, t, h, a)
-            epilogue(acc, t, h)
+                mm(acc, t, 0, a, a == 0, a == 2)
+            epilogue(acc, t, 0)
+        for t in range(TILES):
+            acc = psum.tile([P, NH], F32, name="acc", tag="acc")
+            for a in (2, 0, 1):
+                mm(acc, t, 1, a, a == 2, a == 1)
+            epilogue(acc, t, 1)

@@ -71,17 +71,17 @@ def tile_list_tabo_tm_silu_kernel(tc, tab, w8, w4_words, w4_scales, b, offs, out
 
         nc.sync.dma_start(offsets[:], offs)
         nc.sync.dma_start(out=bvec[:], in_=b.rearrange("(p c) -> p c", c=8))
-        nc.sync.dma_start(out=w4w[:].bitcast(I32), in_=w4_words[0].bitcast(I32))
         words0 = slot("slot_words", [P, T], I32, "words0")
         load_words(words0, 0)
-        for q in range(3):
+        nc.sync.dma_start(out=w4w[:].bitcast(I32), in_=w4_words[0].bitcast(I32))
+        for q in range(4):
             src = tab[0:2, (512 + 4 * q) * T : (516 + 4 * q) * T].rearrange("a (r t) -> a r t", r=4)
             k = 32 * q + PLANE[0]
-            nc.gpsimd.dma_start(out=planes[k : k + 8, :].bitcast(I32), in_=src.bitcast(I32))
-        for a, q in ((0, 3), (1, 3), (2, 0), (2, 1), (2, 2), (2, 3)):
-            src = tab[a, (512 + 4 * q) * T : (516 + 4 * q) * T].rearrange("(r t) -> r t", r=4)
-            k = 32 * q + PLANE[a]
-            nc.sync.dma_start(out=planes[k : k + 4, :].bitcast(I32), in_=src.bitcast(I32))
+            queue = nc.gpsimd if q < 3 else nc.sync
+            queue.dma_start(out=planes[k : k + 8, :].bitcast(I32), in_=src.bitcast(I32))
+        rows2 = tab[2, 512 * T : 528 * T].rearrange("(g t) -> g t", g=16)
+        for r in range(4):
+            nc.sync.dma_start(out=planes[r:P:32, :].bitcast(I32), in_=rows2[r:16:4, :].bitcast(I32))
 
         make_identity(nc, ident[:])
         for u in range(2):
@@ -98,10 +98,8 @@ def tile_list_tabo_tm_silu_kernel(tc, tab, w8, w4_words, w4_scales, b, offs, out
         load_words(words2, 2)
         w4s = placed(4 * T, [P, M], U8, "w4s")
         nc.vector.memset(w4s[:].bitcast(I32), 0)
-        for q in range(4):
-            nc.sync.dma_start(
-                out=w4s[32 * q : 32 * q + 4, :].bitcast(I32), in_=w4_scales[0, 4 * q : 4 * q + 4, :].bitcast(I32)
-            )
+        for r in range(4):
+            nc.sync.dma_start(out=w4s[r:P:32, :].bitcast(I32), in_=w4_scales[0, r:16:4, :].bitcast(I32))
 
         def interleave(engine, dst, src):
             src = src.rearrange("p j w -> p w j")
@@ -142,12 +140,13 @@ def tile_list_tabo_tm_silu_kernel(tc, tab, w8, w4_words, w4_scales, b, offs, out
                 stop=stop,
             )
 
-        def epilogue(acc, t, h):
-            z = zpool.tile([P, NH], F32, name="z")
-            nc.vector.tensor_tensor(out=z[:], in0=acc[:], in1=bias[:, NH * h : NH * (h + 1)], op=ADD)
-            y = ypool.tile([P, NH], F32, name="y")
+        def epilogue(acc, t, h, lo=0, hi=NH):
+            cols = slice(NH * h + lo, NH * h + hi)
+            z = zpool.tile([P, hi - lo], F32, name="z")
+            nc.vector.tensor_tensor(out=z[:], in0=acc[:, lo:hi], in1=bias[:, cols], op=ADD)
+            y = ypool.tile([P, hi - lo], F32, name="y")
             nc.scalar.activation(y[:], z[:], SILU)
-            nc.sync.dma_start(out=out[t * P : (t + 1) * P, NH * h : NH * (h + 1)], in_=y[:])
+            nc.sync.dma_start(out=out[t * P : (t + 1) * P, cols], in_=y[:])
 
         gather_words(gwords[0][:], words0, 0, S)
         words1 = slot("slot_words", [P, T], I32, "words1")
@@ -199,4 +198,8 @@ def tile_list_tabo_tm_silu_kernel(tc, tab, w8, w4_words, w4_scales, b, offs, out
             acc = psum.tile([P, NH], F32, name="acc", tag="acc")
             for a in (2, 0, 1):
                 mm(acc, t, 1, a, a == 2, a == 1)
-            epilogue(acc, t, 1)
+            if t < TILES - 1:
+                epilogue(acc, t, 1)
+            else:
+                epilogue(acc, t, 1, 0, NQ)
+                epilogue(acc, t, 1, NQ, NH)

@@ -30,36 +30,33 @@ def tile_list_tabo_tm_silu_kernel(tc, tab, w8, w4_words, w4_scales, b, offs, out
     with ExitStack() as ctx:
         keep = ctx.enter_context(tc.tile_pool(name="keep", bufs=1))
         stage = ctx.enter_context(tc.tile_pool(name="stage", bufs=1))
-        zpool = ctx.enter_context(tc.tile_pool(name="zpool", bufs=6))
-        ypool = ctx.enter_context(tc.tile_pool(name="ypool", bufs=8))
+        zpool = ctx.enter_context(tc.tile_pool(name="zpool", bufs=10))
+        ypool = ctx.enter_context(tc.tile_pool(name="ypool", bufs=25))
         psum = ctx.enter_context(tc.psum_pool(name="psum", bufs=8))
 
         def slot(tag, shape, dtype, name):
-            return keep.tile(shape, dtype, name=name, tag=tag, align_bytes=64)
+            return keep.tile(shape, dtype, name=name, tag=tag, align_bytes=256)
 
         def placed(offset, shape, dtype, name):
-            return stage.tile(shape, dtype, name=name, align_bytes=64, offset=offset)
+            return stage.tile(shape, dtype, name=name, align_bytes=256, offset=offset)
 
         offsets = keep.tile([P, S // 16], U16, name="offsets")
-        gwords = {a: keep.tile([P, S], U32, name=f"gwords{a}", align_bytes=64) for a in (0, 2)}
-        gwords[1] = keep.tile([P, AHEAD * P], U32, name="gwords1", align_bytes=64)
-        gplanes = keep.tile([P, S], U8, name="gplanes", align_bytes=64)
+        gwords = {a: keep.tile([P, S], U32, name=f"gwords{a}", align_bytes=256) for a in (0, 2)}
+        gwords[1] = keep.tile([P, AHEAD * P], U32, name="gwords1", align_bytes=256)
+        gplanes = keep.tile([P, S], U8, name="gplanes", align_bytes=256)
         codes = {}
         wscale = {}
         for h in range(2):
             for a in range(2):
-                codes[h, a] = keep.tile([P, NH], U32, name=f"codes{h}{a}", align_bytes=64)
-                wscale[h, a] = keep.tile([P, NH], U8, name=f"wscale{h}{a}", align_bytes=64)
-        w4w = keep.tile([P, 2 * M], U8, name="w4w", align_bytes=64)
-        bias = keep.tile([P, M], F32, name="bias")
-        warm = keep.tile([P, 1], F32, name="warm")
-        planes = keep.tile([P, T], U8, name="planes", align_bytes=64)
+                codes[h, a] = keep.tile([P, NH], U32, name=f"codes{h}{a}", align_bytes=256)
+                wscale[h, a] = keep.tile([P, NH], U8, name=f"wscale{h}{a}", align_bytes=256)
+        w4w = keep.tile([P, 2 * M], U8, name="w4w", align_bytes=256)
+        bias = keep.tile([P, M], F32, name="bias", align_bytes=256)
+        planes = keep.tile([P, T], U8, name="planes", align_bytes=256)
         bvec = slot("slot_a", [P, 8], F32, "bvec")
         ident = placed(4 * T - 256, [P, P], F32, "ident")
 
         nc.vector.memset(planes[:].bitcast(I32), 0)
-        nc.vector.memset(warm[:], 0.0)
-        nc.scalar.activation(warm[:], warm[:], SILU)
 
         def load_w8(dst, a, lo, hi):
             src = w8[512 * a : 512 * (a + 1), lo:hi]
@@ -142,9 +139,9 @@ def tile_list_tabo_tm_silu_kernel(tc, tab, w8, w4_words, w4_scales, b, offs, out
 
         def epilogue(acc, t, h, lo=0, hi=NH):
             cols = slice(NH * h + lo, NH * h + hi)
-            z = zpool.tile([P, hi - lo], F32, name="z")
+            z = zpool.tile([P, hi - lo], F32, name="z", align_bytes=256)
             nc.vector.tensor_tensor(out=z[:], in0=acc[:, lo:hi], in1=bias[:, cols], op=ADD)
-            y = ypool.tile([P, hi - lo], F32, name="y")
+            y = ypool.tile([P, hi - lo], F32, name="y", align_bytes=256)
             nc.scalar.activation(y[:], z[:], SILU)
             nc.sync.dma_start(out=out[t * P : (t + 1) * P, cols], in_=y[:])
 
@@ -152,7 +149,7 @@ def tile_list_tabo_tm_silu_kernel(tc, tab, w8, w4_words, w4_scales, b, offs, out
         words1 = slot("slot_words", [P, T], I32, "words1")
         load_words(words1, 1)
         nc.vector.tensor_copy(gplanes[:], planes[:].indirect(offsets[:]))
-        grouped00 = keep.tile([P, NH, 4], BF16, name="grouped00", align_bytes=64)
+        grouped00 = keep.tile([P, NH, 4], BF16, name="grouped00", align_bytes=256)
         interleave("scalar", grouped00[:], raw00[:])
         quantize(0, 0, grouped00[:], 0, NH)
         raw01 = slot("slot_a", [P, 2, 4, NQ], F32, "raw01")
@@ -176,13 +173,12 @@ def tile_list_tabo_tm_silu_kernel(tc, tab, w8, w4_words, w4_scales, b, offs, out
         quantize(0, 1, quarter0[:], 0, NQ)
         gwords["late"] = slot("slot_q", [P, S - AHEAD * P], U32, "gwords1late")
         gather_words(gwords["late"][:], words1, AHEAD * P, S)
-        quarter1 = keep.tile([P, NQ, 4], BF16, name="quarter1", align_bytes=64)
+        quarter1 = slot("slot_h", [P, NQ, 4], BF16, "quarter1")
         interleave("scalar", quarter1[:], raw01[:, 1])
         quantize(0, 1, quarter1[:], NQ, NH)
         for a in range(2):
-            grouped = keep.tile([P, NH, 4], BF16, name=f"grouped1{a}", align_bytes=64)
-            for lo in range(0, NH, 128):
-                interleave("gpsimd", grouped[:, lo : lo + 128, :], raw1[:, a, :, lo : lo + 128])
+            grouped = slot("slot_h", [P, NH, 4], BF16, f"grouped1{a}")
+            interleave("gpsimd", grouped[:], raw1[:, a])
             quantize(1, a, grouped[:], 0, NH)
         for t in range(AHEAD):
             mm(accs[t], t, 0, 1, False, False, 0, NQ)

@@ -23,6 +23,9 @@ PLANE = (4, 8, 0)
 TILES = S // P
 AHEAD = 8
 NQ = NH // 2
+PAIRS = TILES // 2
+KB = 1024
+CHUNKS = tuple((lo, lo + NQ) for lo in range(0, M, NQ))
 
 
 def tile_list_tabo_tm_silu_kernel(tc, tab, w8, w4_words, w4_scales, b, offs, out):
@@ -46,20 +49,27 @@ def tile_list_tabo_tm_silu_kernel(tc, tab, w8, w4_words, w4_scales, b, offs, out
         gplanes = keep.tile([P, S], U8, name="gplanes", align_bytes=256)
         codes = {}
         wscale = {}
-        for h in range(2):
+        for c in range(2):
             for a in range(2):
-                codes[h, a] = keep.tile([P, NH], U32, name=f"codes{h}{a}", align_bytes=256)
-                wscale[h, a] = keep.tile([P, NH], U8, name=f"wscale{h}{a}", align_bytes=256)
-        w4w = keep.tile([P, 2 * M], U8, name="w4w", align_bytes=256)
+                if (c, a) != (0, 0):
+                    codes[c, a] = keep.tile([P, NQ], U32, name=f"codes{c}{a}", align_bytes=256)[:]
+                wscale[c, a] = keep.tile([P, NQ], U8, name=f"wscale{c}{a}", align_bytes=256)[:]
+        for c in range(2, 4):
+            codes[c] = keep.tile([P, 2 * NQ], U32, name=f"codes{c}", align_bytes=256)
+            wscale[c] = keep.tile([P, 2 * NQ], U8, name=f"wscale{c}", align_bytes=256)
+            for a in range(2):
+                codes[c, a] = codes[c][:, a * NQ : (a + 1) * NQ]
+                wscale[c, a] = wscale[c][:, a * NQ : (a + 1) * NQ]
+        w4w = {0: keep.tile([P, M], U8, name="w4w0", align_bytes=256)}
         bias = keep.tile([P, M], F32, name="bias", align_bytes=256)
-        planes = keep.tile([P, T], U8, name="planes", align_bytes=256)
+        planes = slot("slot_planes", [P, T], U8, "planes")
         bvec = slot("slot_a", [P, 8], F32, "bvec")
-        ident = placed(4 * T - 256, [P, P], F32, "ident")
+        ident = placed(17 * KB - 256, [P, P], F32, "ident")
 
         nc.vector.memset(planes[:].bitcast(I32), 0)
 
-        def load_w8(dst, a, lo, hi):
-            src = w8[512 * a : 512 * (a + 1), lo:hi]
+        def load_w8(dst, a, c):
+            src = w8[512 * a : 512 * (a + 1), CHUNKS[c][0] : CHUNKS[c][1]]
             nc.sync.dma_start(out=dst, in_=src.rearrange("(p j) w -> p j w", j=4))
 
         def load_words(words, a):
@@ -70,7 +80,7 @@ def tile_list_tabo_tm_silu_kernel(tc, tab, w8, w4_words, w4_scales, b, offs, out
         nc.sync.dma_start(out=bvec[:], in_=b.rearrange("(p c) -> p c", c=8))
         words0 = slot("slot_words", [P, T], I32, "words0")
         load_words(words0, 0)
-        nc.sync.dma_start(out=w4w[:].bitcast(I32), in_=w4_words[0].bitcast(I32))
+        nc.sync.dma_start(out=w4w[0][:].bitcast(I32), in_=w4_words[0, :, 0:M].bitcast(I32))
         for q in range(4):
             src = tab[0:2, (512 + 4 * q) * T : (516 + 4 * q) * T].rearrange("a (r t) -> a r t", r=4)
             k = 32 * q + PLANE[0]
@@ -89,58 +99,68 @@ def tile_list_tabo_tm_silu_kernel(tc, tab, w8, w4_words, w4_scales, b, offs, out
             dst = bias[:].rearrange("q (p c) -> q p c", c=8)[:, :, 4 * u : 4 * u + 4]
             nc.scalar.copy(dst, pb[:].rearrange("q c p -> q p c"))
 
-        raw00 = slot("slot_a", [P, 4, NH], F32, "raw00")
-        load_w8(raw00[:], 0, 0, NH)
-        words2 = placed(0, [P, T], I32, "words2")
+        raw00 = slot("slot_a", [P, 4, NQ], F32, "raw00")
+        load_w8(raw00[:], 0, 0)
+        words2 = placed(KB, [P, T], I32, "words2")
         load_words(words2, 2)
-        w4s = placed(4 * T, [P, M], U8, "w4s")
+        w4s = placed(17 * KB, [P, M], U8, "w4s")
         nc.vector.memset(w4s[:].bitcast(I32), 0)
         for r in range(4):
             nc.sync.dma_start(out=w4s[r:P:32, :].bitcast(I32), in_=w4_scales[0, r:16:4, :].bitcast(I32))
 
         def interleave(engine, dst, src):
-            src = src.rearrange("p j w -> p w j")
-            if engine == "scalar":
-                nc.scalar.copy(dst, src)
-            else:
-                nc.gpsimd.tensor_scalar(dst, src, 1.0, 0.0, MULT, ADD)
+            nc.scalar.copy(dst, src.rearrange("p j w -> p w j"))
 
-        def quantize(h, a, grouped, lo, hi):
+        def quantize(c, a, grouped):
             nc.vector.quantize_mx(
-                out=codes[h, a][:, lo:hi].bitcast(FP8X4),
-                scales=wscale[h, a][:, lo:hi],
+                out=codes[c, a].bitcast(FP8X4),
+                scales=wscale[c, a],
                 in_=grouped.rearrange("p w j -> p (w j)"),
             )
 
         def gather_words(dst, words, lo, hi):
             nc.vector.tensor_copy(dst, words[:].bitcast(U32).indirect(offsets[:, lo // 16 : hi // 16]))
 
-        def mm(acc, t, h, a, start, stop, lo=0, hi=NH):
+        def mm(acc, t, c, a, lo, hi, start, stop):
             cols = slice(t * P, (t + 1) * P)
-            if a < 2:
-                rhs = codes[h, a][:, lo:hi].bitcast(FP8X4)
-                rhs_scale = wscale[h, a][:, lo:hi]
-            else:
-                rhs = w4w[:, 2 * NH * h : 2 * NH * (h + 1)].bitcast(FP4X4)
-                rhs_scale = w4s[:, NH * h : NH * (h + 1)]
             if a == 1 and t >= AHEAD:
                 lhsT = gwords["late"][:, (t - AHEAD) * P : (t - AHEAD + 1) * P]
             else:
                 lhsT = gwords[a][:, cols]
-            nc.tensor.matmul_mx(
-                out=acc[:, lo:hi],
-                lhsT=lhsT.bitcast(FP8X4),
-                lhsT_scale=gplanes[PLANE[a] : P, cols],
-                rhs=rhs,
-                rhs_scale=rhs_scale,
-                start=start,
-                stop=stop,
-            )
+            step = P if a == 2 and hi - lo < NH else hi - lo
+            for n0 in range(lo, hi, step):
+                if a < 2:
+                    rhs = codes[c, a][:, n0 : n0 + step].bitcast(FP8X4)
+                    rhs_scale = wscale[c, a][:, n0 : n0 + step]
+                else:
+                    n = CHUNKS[c][0] + n0
+                    rhs = w4w[n // NH][:, 2 * (n % NH) : 2 * (n % NH + step)].bitcast(FP4X4)
+                    rhs_scale = w4s[:, n : n + step]
+                nc.tensor.matmul_mx(
+                    out=acc[:, n0 - lo : n0 - lo + step],
+                    lhsT=lhsT.bitcast(FP8X4),
+                    lhsT_scale=gplanes[PLANE[a] : P, cols],
+                    rhs=rhs,
+                    rhs_scale=rhs_scale,
+                    start=start and n0 == lo,
+                    stop=stop and n0 + step == hi,
+                )
 
-        def epilogue(acc, t, h, lo=0, hi=NH):
-            cols = slice(NH * h + lo, NH * h + hi)
+        def pair(acc, u, c, a, start, stop):
+            for i in range(2):
+                mm(acc[:, i, :], 2 * u + i, c, a, 0, NQ, start and i == 0, stop and i == 1)
+
+        def pair_out(acc, u, c, z):
+            cols = slice(CHUNKS[c][0], CHUNKS[c][1])
+            nc.vector.tensor_tensor(out=z[:], in0=acc[:], in1=bias[:, cols].unsqueeze(1).to_broadcast([P, 2, NQ]), op=ADD)
+            y = ypool.tile([P, 2, NQ], F32, name="y", align_bytes=256)
+            nc.scalar.activation(y[:], z[:], SILU)
+            nc.sync.dma_start(out=out[2 * u * P : 2 * (u + 1) * P, cols].rearrange("(i p) n -> p i n", i=2), in_=y[:])
+
+        def epilogue(acc, t, lo, hi):
+            cols = slice(NH + lo, NH + hi)
             z = zpool.tile([P, hi - lo], F32, name="z", align_bytes=256)
-            nc.vector.tensor_tensor(out=z[:], in0=acc[:, lo:hi], in1=bias[:, cols], op=ADD)
+            nc.vector.tensor_tensor(out=z[:], in0=acc, in1=bias[:, cols], op=ADD)
             y = ypool.tile([P, hi - lo], F32, name="y", align_bytes=256)
             nc.scalar.activation(y[:], z[:], SILU)
             nc.sync.dma_start(out=out[t * P : (t + 1) * P, cols], in_=y[:])
@@ -149,53 +169,83 @@ def tile_list_tabo_tm_silu_kernel(tc, tab, w8, w4_words, w4_scales, b, offs, out
         words1 = slot("slot_words", [P, T], I32, "words1")
         load_words(words1, 1)
         nc.vector.tensor_copy(gplanes[:], planes[:].indirect(offsets[:]))
-        grouped00 = keep.tile([P, NH, 4], BF16, name="grouped00", align_bytes=256)
+        grouped00 = placed(21 * KB, [P, NQ, 4], BF16, "grouped00")
         interleave("scalar", grouped00[:], raw00[:])
-        quantize(0, 0, grouped00[:], 0, NH)
-        raw01 = slot("slot_a", [P, 2, 4, NQ], F32, "raw01")
-        for u in range(2):
-            load_w8(raw01[:, u], 1, u * NQ, (u + 1) * NQ)
+        codes[0, 0] = slot("slot_planes", [P, NQ], U32, "codes00")[:]
+        quantize(0, 0, grouped00[:])
+        raw01 = slot("slot_a", [P, 4, NQ], F32, "raw01")
+        load_w8(raw01[:], 1, 0)
+        raw10 = placed(18 * KB, [P, 4, NQ], F32, "raw10")
+        load_w8(raw10[:], 0, 1)
+        raw11 = placed(22 * KB, [P, 4, NQ], F32, "raw11")
+        load_w8(raw11[:], 1, 1)
 
-        accs = [psum.tile([P, NH], F32, name=f"acc{t}", tag="acc") for t in range(AHEAD)]
-        for t in range(AHEAD):
-            mm(accs[t], t, 0, 0, True, False)
-        for lo in range(0, S, 512):
-            gather_words(gwords[2][:, lo : lo + 512], words2, lo, lo + 512)
-        raw1 = placed(0, [P, 2, 4, NH], F32, "raw1")
-        for a in range(2):
-            load_w8(raw1[:, a], a, NH, M)
-        for t in range(AHEAD):
-            mm(accs[t], t, 0, 2, False, False)
+        first = [psum.tile([P, 2, NQ], F32, name=f"first{u}", tag="acc") for u in range(PAIRS)]
+        for u in range(PAIRS):
+            pair(first[u], u, 0, 0, True, False)
+        gather_words(gwords[2][:], words2, 0, S)
+        w4w[1] = placed(16 * KB, [P, M], U8, "w4w1")
+        nc.sync.dma_start(out=w4w[1][:].bitcast(I32), in_=w4_words[0, :, M : 2 * M].bitcast(I32))
+        raw = {c: placed(8 * KB * (c - 2), [P, 2, 4, NQ], F32, f"raw{c}") for c in (2, 3)}
+        for c in (2, 3):
+            for a in range(2):
+                load_w8(raw[c][:, a], a, c)
+        for u in range(PAIRS):
+            pair(first[u], u, 0, 2, False, False)
+        second = [psum.tile([P, 2, NQ], F32, name=f"second{u}", tag="acc") for u in range(2)]
+        for u in range(2):
+            pair(second[u], u, 1, 2, True, False)
         for lo in range(0, AHEAD * P, 512):
             gather_words(gwords[1][:, lo : lo + 512], words1, lo, lo + 512)
-        quarter0 = slot("slot_q", [P, NQ, 4], BF16, "quarter0")
-        interleave("scalar", quarter0[:], raw01[:, 0])
-        quantize(0, 1, quarter0[:], 0, NQ)
+        grouped01 = slot("slot_q", [P, NQ, 4], BF16, "grouped01")
+        interleave("scalar", grouped01[:], raw01[:])
+        quantize(0, 1, grouped01[:])
         gwords["late"] = slot("slot_q", [P, S - AHEAD * P], U32, "gwords1late")
         gather_words(gwords["late"][:], words1, AHEAD * P, S)
-        quarter1 = slot("slot_h", [P, NQ, 4], BF16, "quarter1")
-        interleave("scalar", quarter1[:], raw01[:, 1])
-        quantize(0, 1, quarter1[:], NQ, NH)
-        for a in range(2):
-            grouped = slot("slot_h", [P, NH, 4], BF16, f"grouped1{a}")
-            interleave("gpsimd", grouped[:], raw1[:, a])
-            quantize(1, a, grouped[:], 0, NH)
-        for t in range(AHEAD):
-            mm(accs[t], t, 0, 1, False, False, 0, NQ)
-        for t in range(AHEAD):
-            mm(accs[t], t, 0, 1, False, True, NQ, NH)
-            epilogue(accs[t], t, 0)
-        for t in range(AHEAD, TILES):
-            acc = psum.tile([P, NH], F32, name="acc", tag="acc")
-            for a in range(3):
-                mm(acc, t, 0, a, a == 0, a == 2)
-            epilogue(acc, t, 0)
-        for t in range(TILES):
-            acc = psum.tile([P, NH], F32, name="acc", tag="acc")
-            for a in (2, 0, 1):
-                mm(acc, t, 1, a, a == 2, a == 1)
-            if t < TILES - 1:
-                epilogue(acc, t, 1)
+        grouped10 = slot("slot_z", [P, NQ, 4], BF16, "grouped10")
+        interleave("scalar", grouped10[:], raw10[:])
+        quantize(1, 0, grouped10[:])
+        grouped11 = placed(30 * KB, [P, NQ, 4], BF16, "grouped11")
+        interleave("scalar", grouped11[:], raw11[:])
+        quantize(1, 1, grouped11[:])
+        for c in (2, 3):
+            grouped = placed(27 * KB, [P, 2, NQ, 4], BF16, f"grouped{c}")
+            nc.gpsimd.tensor_scalar(grouped[:], raw[c][:].rearrange("p a j w -> p a w j"), 1.0, 0.0, MULT, ADD)
+            nc.vector.quantize_mx(
+                out=codes[c][:].bitcast(FP8X4),
+                scales=wscale[c][:],
+                in_=grouped[:].rearrange("p a w j -> p (a w j)"),
+            )
+        for u in range(PAIRS):
+            pair(first[u], u, 0, 1, False, True)
+            if u == 0:
+                z = slot("slot_z", [P, 2, NQ], F32, "z0")
+            elif u == 1:
+                z = placed(31 * KB, [P, 2, NQ], F32, "z1")
             else:
-                epilogue(acc, t, 1, 0, NQ)
-                epilogue(acc, t, 1, NQ, NH)
+                z = zpool.tile([P, 2, NQ], F32, name="z", align_bytes=256)
+            pair_out(first[u], u, 0, z)
+        for u in range(PAIRS):
+            if u < 2:
+                acc = second[u]
+            else:
+                acc = psum.tile([P, 2, NQ], F32, name="acc", tag="acc")
+                pair(acc, u, 1, 2, True, False)
+            pair(acc, u, 1, 0, False, False)
+            pair(acc, u, 1, 1, False, True)
+            z = zpool.tile([P, 2, NQ], F32, name="z", align_bytes=256)
+            pair_out(acc, u, 1, z)
+        for c in (2, 3):
+            for u in range(PAIRS):
+                if c == 3 and u == PAIRS - 1:
+                    for t in (2 * u, 2 * u + 1):
+                        acc = psum.tile([P, NQ], F32, name="acc", tag="acc")
+                        for a in (2, 0, 1):
+                            mm(acc[:], t, c, a, 0, NQ, a == 2, a == 1)
+                        epilogue(acc[:], t, NQ, NH)
+                else:
+                    acc = psum.tile([P, 2, NQ], F32, name="acc", tag="acc")
+                    for a in (2, 0, 1):
+                        pair(acc, u, c, a, a == 2, a == 1)
+                    z = zpool.tile([P, 2, NQ], F32, name="z", align_bytes=256)
+                    pair_out(acc, u, c, z)

@@ -19,7 +19,7 @@ P = 128
 O, K, M, T, S = 1024, 1536, 1024, 4096, 1536
 FLOPS = 2 * K * M * S
 NH = 512
-PLANE = (4, 8, 0)
+PLANE = (4, 8, 12)
 TILES = S // P
 AHEAD = 8
 NQ = NH // 2
@@ -47,6 +47,7 @@ def tile_list_tabo_tm_silu_kernel(tc, tab, w8, w4_words, w4_scales, b, offs, out
         gwords = {a: keep.tile([P, S], U32, name=f"gwords{a}", align_bytes=256) for a in (0, 2)}
         gwords[1] = keep.tile([P, AHEAD * P], U32, name="gwords1", align_bytes=256)
         gplanes = keep.tile([P, S], U8, name="gplanes", align_bytes=256)
+        gplane2 = keep.tile([P, S], U8, name="gplane2", align_bytes=256)
         codes = {}
         wscale = {}
         for c in range(2):
@@ -63,10 +64,13 @@ def tile_list_tabo_tm_silu_kernel(tc, tab, w8, w4_words, w4_scales, b, offs, out
         w4w = {0: keep.tile([P, M], U8, name="w4w0", align_bytes=256)}
         bias = keep.tile([P, M], F32, name="bias", align_bytes=256)
         planes = slot("slot_planes", [P, T], U8, "planes")
-        bvec = slot("slot_a", [P, 8], F32, "bvec")
+        bvec = keep.tile([P, 8], F32, name="bvec", align_bytes=256)
         ident = placed(17 * KB - 256, [P, P], F32, "ident")
+        w4s = keep.tile([P, M], U8, name="w4s", align_bytes=256)
 
         nc.vector.memset(planes[:].bitcast(I32), 0)
+        nc.vector.memset(w4s[:].bitcast(I32), 0)
+        nc.vector.memset(gplane2[:].bitcast(I32), 0)
 
         def load_w8(dst, a, c):
             src = w8[512 * a : 512 * (a + 1), CHUNKS[c][0] : CHUNKS[c][1]]
@@ -76,19 +80,14 @@ def tile_list_tabo_tm_silu_kernel(tc, tab, w8, w4_words, w4_scales, b, offs, out
             src = tab[a, 0 : 512 * T].rearrange("(p x) -> p x", p=P)
             nc.sync.dma_start(out=words[:], in_=src.bitcast(I32))
 
-        nc.sync.dma_start(offsets[:], offs)
         nc.sync.dma_start(out=bvec[:], in_=b.rearrange("(p c) -> p c", c=8))
         words0 = slot("slot_words", [P, T], I32, "words0")
         load_words(words0, 0)
-        nc.sync.dma_start(out=w4w[0][:].bitcast(I32), in_=w4_words[0, :, 0:M].bitcast(I32))
+        nc.sync.dma_start(offsets[:], offs)
         for q in range(4):
-            src = tab[0:2, (512 + 4 * q) * T : (516 + 4 * q) * T].rearrange("a (r t) -> a r t", r=4)
+            src = tab[:, (512 + 4 * q) * T : (516 + 4 * q) * T].rearrange("a (r t) -> a r t", r=4)
             k = 32 * q + PLANE[0]
-            queue = nc.gpsimd if q < 3 else nc.sync
-            queue.dma_start(out=planes[k : k + 8, :].bitcast(I32), in_=src.bitcast(I32))
-        rows2 = tab[2, 512 * T : 528 * T].rearrange("(g t) -> g t", g=16)
-        for r in range(4):
-            nc.sync.dma_start(out=planes[r:P:32, :].bitcast(I32), in_=rows2[r:16:4, :].bitcast(I32))
+            nc.gpsimd.dma_start(out=planes[k : k + 12, :].bitcast(I32), in_=src.bitcast(I32))
 
         make_identity(nc, ident[:])
         for u in range(2):
@@ -103,8 +102,7 @@ def tile_list_tabo_tm_silu_kernel(tc, tab, w8, w4_words, w4_scales, b, offs, out
         load_w8(raw00[:], 0, 0)
         words2 = placed(KB, [P, T], I32, "words2")
         load_words(words2, 2)
-        w4s = placed(17 * KB, [P, M], U8, "w4s")
-        nc.vector.memset(w4s[:].bitcast(I32), 0)
+        nc.sync.dma_start(out=w4w[0][:].bitcast(I32), in_=w4_words[0, :, 0:M].bitcast(I32))
         for r in range(4):
             nc.sync.dma_start(out=w4s[r:P:32, :].bitcast(I32), in_=w4_scales[0, r:16:4, :].bitcast(I32))
 
@@ -139,7 +137,7 @@ def tile_list_tabo_tm_silu_kernel(tc, tab, w8, w4_words, w4_scales, b, offs, out
                 nc.tensor.matmul_mx(
                     out=acc[:, n0 - lo : n0 - lo + step],
                     lhsT=lhsT.bitcast(FP8X4),
-                    lhsT_scale=gplanes[PLANE[a] : P, cols],
+                    lhsT_scale=gplanes[PLANE[a] : P, cols] if a < 2 else gplane2[:, cols],
                     rhs=rhs,
                     rhs_scale=rhs_scale,
                     start=start and n0 == lo,
@@ -169,6 +167,8 @@ def tile_list_tabo_tm_silu_kernel(tc, tab, w8, w4_words, w4_scales, b, offs, out
         words1 = slot("slot_words", [P, T], I32, "words1")
         load_words(words1, 1)
         nc.vector.tensor_copy(gplanes[:], planes[:].indirect(offsets[:]))
+        for r in range(4):
+            nc.scalar.dma_start(out=gplane2[r:P:32, :].bitcast(I32), in_=gplanes[PLANE[2] + r : P : 32, :].bitcast(I32))
         grouped00 = placed(21 * KB, [P, NQ, 4], BF16, "grouped00")
         interleave("scalar", grouped00[:], raw00[:])
         codes[0, 0] = slot("slot_planes", [P, NQ], U32, "codes00")[:]

@@ -107,7 +107,7 @@ def tile_list_tabo_tm_silu_kernel(tc, tab, w8, w4_words, w4_scales, b, offs, out
             nc.sync.dma_start(out=w4s[r:P:32, :].bitcast(I32), in_=w4_scales[0, r:16:4, :].bitcast(I32))
 
         def interleave(engine, dst, src):
-            nc.scalar.copy(dst, src.rearrange("p j w -> p w j"))
+            nc.scalar.copy(dst.rearrange("p (c i) j -> p c j i", i=4), src.rearrange("p j (c i) -> p c j i", i=4))
 
         def quantize(c, a, grouped):
             nc.vector.quantize_mx(

@@ -1,7 +1,6 @@
 from contextlib import ExitStack
 
 import concourse.mybir as mybir
-from concourse.masks import make_identity
 
 F32 = mybir.dt.float32
 BF16 = mybir.dt.bfloat16
@@ -18,14 +17,15 @@ SILU = mybir.ActivationFunctionType.Silu
 P = 128
 O, K, M, T, S = 1024, 1536, 1024, 4096, 1536
 FLOPS = 2 * K * M * S
-NH = 512
+CHUNK = 256
 PLANE = (4, 8, 12)
 TILES = S // P
-AHEAD = 8
-NQ = NH // 2
 PAIRS = TILES // 2
+BANKS = 8
+SLICE = 512
+HELD = 2
+EARLY = 2
 KB = 1024
-CHUNKS = tuple((lo, lo + NQ) for lo in range(0, M, NQ))
 
 
 def tile_list_tabo_tm_silu_kernel(tc, tab, w8, w4_words, w4_scales, b, offs, out):
@@ -35,217 +35,252 @@ def tile_list_tabo_tm_silu_kernel(tc, tab, w8, w4_words, w4_scales, b, offs, out
         stage = ctx.enter_context(tc.tile_pool(name="stage", bufs=1))
         zpool = ctx.enter_context(tc.tile_pool(name="zpool", bufs=10))
         ypool = ctx.enter_context(tc.tile_pool(name="ypool", bufs=25))
-        psum = ctx.enter_context(tc.psum_pool(name="psum", bufs=8))
+        psum = ctx.enter_context(tc.psum_pool(name="psum", bufs=BANKS))
 
-        def slot(tag, shape, dtype, name):
-            return keep.tile(shape, dtype, name=name, tag=tag, align_bytes=256)
+        def kept(shape, dtype, name, tag=None):
+            return keep.tile(shape, dtype, name=name, tag=tag or name, align_bytes=256)
 
         def placed(offset, shape, dtype, name):
             return stage.tile(shape, dtype, name=name, align_bytes=256, offset=offset)
 
+        def columns(c):
+            return slice(c * CHUNK, (c + 1) * CHUNK)
+
         offsets = keep.tile([P, S // 16], U16, name="offsets")
-        gwords = {a: keep.tile([P, S], U32, name=f"gwords{a}", align_bytes=256) for a in (0, 2)}
-        gwords[1] = keep.tile([P, AHEAD * P], U32, name="gwords1", align_bytes=256)
-        gplanes = keep.tile([P, S], U8, name="gplanes", align_bytes=256)
-        gplane2 = keep.tile([P, S], U8, name="gplane2", align_bytes=256)
-        codes = {}
-        wscale = {}
-        for c in range(2):
-            for a in range(2):
-                if (c, a) != (0, 0):
-                    codes[c, a] = keep.tile([P, NQ], U32, name=f"codes{c}{a}", align_bytes=256)[:]
-                wscale[c, a] = keep.tile([P, NQ], U8, name=f"wscale{c}{a}", align_bytes=256)[:]
-        for c in range(2, 4):
-            codes[c] = keep.tile([P, 2 * NQ], U32, name=f"codes{c}", align_bytes=256)
-            wscale[c] = keep.tile([P, 2 * NQ], U8, name=f"wscale{c}", align_bytes=256)
-            for a in range(2):
-                codes[c, a] = codes[c][:, a * NQ : (a + 1) * NQ]
-                wscale[c, a] = wscale[c][:, a * NQ : (a + 1) * NQ]
-        w4w = {0: keep.tile([P, M], U8, name="w4w0", align_bytes=256)}
-        bias = keep.tile([P, M], F32, name="bias", align_bytes=256)
-        planes = slot("slot_planes", [P, T], U8, "planes")
-        bvec = keep.tile([P, 8], F32, name="bvec", align_bytes=256)
-        ident = placed(17 * KB - 256, [P, P], F32, "ident")
-        w4s = keep.tile([P, M], U8, name="w4s", align_bytes=256)
+        planes = placed(44 * KB, [P, T], U8, "planes")
+        w4_plane = kept([P, M], U8, "w4_plane")
+        picked_planes = kept([P, S], U8, "picked_planes")
+        picked_plane2 = kept([P, S], U8, "picked_plane2")
+        bias_cols = kept([P, 8], F32, "bias_cols")
+        bias = kept([P, M], F32, "bias")
+        ident = kept([P, P], F32, "ident")
+        zeros = placed(17 * KB - 256, [P, P], F32, "zeros")
 
+        nc.vector.memset(w4_plane[:].bitcast(I32), 0)
+        nc.vector.memset(zeros[:], 0.0)
         nc.vector.memset(planes[:].bitcast(I32), 0)
-        nc.vector.memset(w4s[:].bitcast(I32), 0)
-        nc.vector.memset(gplane2[:].bitcast(I32), 0)
+        nc.vector.memset(picked_plane2[:].bitcast(I32), 0)
 
-        def load_w8(dst, a, c):
-            src = w8[512 * a : 512 * (a + 1), CHUNKS[c][0] : CHUNKS[c][1]]
-            nc.sync.dma_start(out=dst, in_=src.rearrange("(p j) w -> p j w", j=4))
+        w4_codes = {}
+        codes = {}
+        scales = {}
+        picked = {}
+        sums = {}
 
-        def load_words(words, a):
+        def load_table(words, a):
             src = tab[a, 0 : 512 * T].rearrange("(p x) -> p x", p=P)
             nc.sync.dma_start(out=words[:], in_=src.bitcast(I32))
 
-        nc.sync.dma_start(out=bvec[:], in_=b.rearrange("(p c) -> p c", c=8))
-        words0 = slot("slot_words", [P, T], I32, "words0")
-        load_words(words0, 0)
-        nc.sync.dma_start(offsets[:], offs)
-        for q in range(4):
-            src = tab[:, (512 + 4 * q) * T : (516 + 4 * q) * T].rearrange("a (r t) -> a r t", r=4)
-            k = 32 * q + PLANE[0]
-            nc.gpsimd.dma_start(out=planes[k : k + 12, :].bitcast(I32), in_=src.bitcast(I32))
+        def load_w8(raw, a, cols):
+            src = w8[512 * a : 512 * (a + 1), cols]
+            nc.sync.dma_start(out=raw, in_=src.rearrange("(p j) w -> p j w", j=4))
 
-        make_identity(nc, ident[:])
-        for u in range(2):
-            pb = psum.tile([P, 4, P], F32, name="pb", tag="acc")
-            for c in range(4):
-                col = bvec[:, 4 * u + c : 4 * u + c + 1].to_broadcast([P, P])
-                nc.tensor.transpose(pb[:, c, :], col, ident[:])
-            dst = bias[:].rearrange("q (p c) -> q p c", c=8)[:, :, 4 * u : 4 * u + 4]
-            nc.scalar.copy(dst, pb[:].rearrange("q c p -> q p c"))
+        def load_w4(words, c, chunks):
+            src = w4_words[0, :, 2 * CHUNK * c : 2 * CHUNK * (c + chunks)]
+            nc.sync.dma_start(out=words[:].bitcast(I32), in_=src.bitcast(I32))
+            for i in range(chunks):
+                w4_codes[c + i] = words[:, 2 * CHUNK * i : 2 * CHUNK * (i + 1)]
 
-        raw00 = slot("slot_a", [P, 4, NQ], F32, "raw00")
-        load_w8(raw00[:], 0, 0)
-        words2 = placed(KB, [P, T], I32, "words2")
-        load_words(words2, 2)
-        nc.sync.dma_start(out=w4w[0][:].bitcast(I32), in_=w4_words[0, :, 0:M].bitcast(I32))
-        for r in range(4):
-            nc.sync.dma_start(out=w4s[r:P:32, :].bitcast(I32), in_=w4_scales[0, r:16:4, :].bitcast(I32))
-
-        def interleave(engine, dst, src):
-            nc.scalar.copy(dst.rearrange("p (c i) j -> p c j i", i=4), src.rearrange("p j (c i) -> p c j i", i=4))
-
-        def quantize(c, a, grouped):
-            nc.vector.quantize_mx(
-                out=codes[c, a].bitcast(FP8X4),
-                scales=wscale[c, a],
-                in_=grouped.rearrange("p w j -> p (w j)"),
-            )
-
-        def gather_words(dst, words, lo, hi):
+        def gather(dst, words, lo, hi):
             nc.vector.tensor_copy(dst, words[:].bitcast(U32).indirect(offsets[:, lo // 16 : hi // 16]))
 
-        def mm(acc, t, c, a, lo, hi, start, stop):
-            cols = slice(t * P, (t + 1) * P)
-            if a == 1 and t >= AHEAD:
-                lhsT = gwords["late"][:, (t - AHEAD) * P : (t - AHEAD + 1) * P]
-            else:
-                lhsT = gwords[a][:, cols]
-            step = P if a == 2 and hi - lo < NH else hi - lo
-            for n0 in range(lo, hi, step):
-                if a < 2:
-                    rhs = codes[c, a][:, n0 : n0 + step].bitcast(FP8X4)
-                    rhs_scale = wscale[c, a][:, n0 : n0 + step]
-                else:
-                    n = CHUNKS[c][0] + n0
-                    rhs = w4w[n // NH][:, 2 * (n % NH) : 2 * (n % NH + step)].bitcast(FP4X4)
-                    rhs_scale = w4s[:, n : n + step]
-                nc.tensor.matmul_mx(
-                    out=acc[:, n0 - lo : n0 - lo + step],
-                    lhsT=lhsT.bitcast(FP8X4),
-                    lhsT_scale=gplanes[PLANE[a] : P, cols] if a < 2 else gplane2[:, cols],
-                    rhs=rhs,
-                    rhs_scale=rhs_scale,
-                    start=start and n0 == lo,
-                    stop=stop and n0 + step == hi,
-                )
-
-        def pair(acc, u, c, a, start, stop):
-            for i in range(2):
-                mm(acc[:, i, :], 2 * u + i, c, a, 0, NQ, start and i == 0, stop and i == 1)
-
-        def pair_out(acc, u, c, z):
-            cols = slice(CHUNKS[c][0], CHUNKS[c][1])
-            nc.vector.tensor_tensor(out=z[:], in0=acc[:], in1=bias[:, cols].unsqueeze(1).to_broadcast([P, 2, NQ]), op=ADD)
-            y = ypool.tile([P, 2, NQ], F32, name="y", align_bytes=256)
-            nc.scalar.activation(y[:], z[:], SILU)
-            nc.sync.dma_start(out=out[2 * u * P : 2 * (u + 1) * P, cols].rearrange("(i p) n -> p i n", i=2), in_=y[:])
-
-        def epilogue(acc, t, lo, hi):
-            cols = slice(NH + lo, NH + hi)
-            z = zpool.tile([P, hi - lo], F32, name="z", align_bytes=256)
-            nc.vector.tensor_tensor(out=z[:], in0=acc, in1=bias[:, cols], op=ADD)
-            y = ypool.tile([P, hi - lo], F32, name="y", align_bytes=256)
-            nc.scalar.activation(y[:], z[:], SILU)
-            nc.sync.dma_start(out=out[t * P : (t + 1) * P, cols], in_=y[:])
-
-        gather_words(gwords[0][:], words0, 0, S)
-        words1 = slot("slot_words", [P, T], I32, "words1")
-        load_words(words1, 1)
-        nc.vector.tensor_copy(gplanes[:], planes[:].indirect(offsets[:]))
-        for r in range(4):
-            nc.scalar.dma_start(out=gplane2[r:P:32, :].bitcast(I32), in_=gplanes[PLANE[2] + r : P : 32, :].bitcast(I32))
-        grouped00 = placed(21 * KB, [P, NQ, 4], BF16, "grouped00")
-        interleave("scalar", grouped00[:], raw00[:])
-        codes[0, 0] = slot("slot_planes", [P, NQ], U32, "codes00")[:]
-        quantize(0, 0, grouped00[:])
-        raw01 = slot("slot_a", [P, 4, NQ], F32, "raw01")
-        load_w8(raw01[:], 1, 0)
-        raw10 = placed(18 * KB, [P, 4, NQ], F32, "raw10")
-        load_w8(raw10[:], 0, 1)
-        raw11 = placed(22 * KB, [P, 4, NQ], F32, "raw11")
-        load_w8(raw11[:], 1, 1)
-
-        first = [psum.tile([P, 2, NQ], F32, name=f"first{u}", tag="acc") for u in range(PAIRS)]
-        for u in range(PAIRS):
-            pair(first[u], u, 0, 0, True, False)
-        gather_words(gwords[2][:], words2, 0, S)
-        w4w[1] = placed(16 * KB, [P, M], U8, "w4w1")
-        nc.sync.dma_start(out=w4w[1][:].bitcast(I32), in_=w4_words[0, :, M : 2 * M].bitcast(I32))
-        raw = {c: placed(8 * KB * (c - 2), [P, 2, 4, NQ], F32, f"raw{c}") for c in (2, 3)}
-        for c in (2, 3):
-            for a in range(2):
-                load_w8(raw[c][:, a], a, c)
-        for u in range(PAIRS):
-            pair(first[u], u, 0, 2, False, False)
-        second = [psum.tile([P, 2, NQ], F32, name=f"second{u}", tag="acc") for u in range(2)]
-        for u in range(2):
-            pair(second[u], u, 1, 2, True, False)
-        for lo in range(0, AHEAD * P, 512):
-            gather_words(gwords[1][:, lo : lo + 512], words1, lo, lo + 512)
-        grouped01 = slot("slot_q", [P, NQ, 4], BF16, "grouped01")
-        interleave("scalar", grouped01[:], raw01[:])
-        quantize(0, 1, grouped01[:])
-        gwords["late"] = slot("slot_q", [P, S - AHEAD * P], U32, "gwords1late")
-        gather_words(gwords["late"][:], words1, AHEAD * P, S)
-        grouped10 = slot("slot_z", [P, NQ, 4], BF16, "grouped10")
-        interleave("scalar", grouped10[:], raw10[:])
-        quantize(1, 0, grouped10[:])
-        grouped11 = placed(30 * KB, [P, NQ, 4], BF16, "grouped11")
-        interleave("scalar", grouped11[:], raw11[:])
-        quantize(1, 1, grouped11[:])
-        for c in (2, 3):
-            grouped = placed(27 * KB, [P, 2, NQ, 4], BF16, f"grouped{c}")
-            nc.gpsimd.tensor_scalar(grouped[:], raw[c][:].rearrange("p a j w -> p a w j"), 1.0, 0.0, MULT, ADD)
-            nc.vector.quantize_mx(
-                out=codes[c][:].bitcast(FP8X4),
-                scales=wscale[c][:],
-                in_=grouped[:].rearrange("p a w j -> p (a w j)"),
+        def interleave_on_scalar(grouped, raw):
+            nc.scalar.copy(
+                grouped.rearrange("p (c i) j -> p c j i", i=4),
+                raw.rearrange("p j (c i) -> p c j i", i=4),
             )
+
+        def quantize(c, passes, grouped, words=None, scales_tag=None):
+            name = f"{c}{passes[0]}"
+            if words is None:
+                words = kept([P, len(passes) * CHUNK], U32, "codes" + name)
+            plane = kept([P, len(passes) * CHUNK], U8, "scales" + name, tag=scales_tag)
+            nc.vector.quantize_mx(out=words[:].bitcast(FP8X4), scales=plane[:], in_=grouped)
+            for i, a in enumerate(passes):
+                codes[c, a] = words[:, columns(i)]
+                scales[c, a] = plane[:, columns(i)]
+
+        def matmul(acc, t, c, a, start, stop):
+            tokens = slice(t * P, (t + 1) * P)
+            if a == 1 and t * P >= 2 * SLICE:
+                lhsT = picked["late"][:, t * P - 2 * SLICE : (t + 1) * P - 2 * SLICE]
+            else:
+                lhsT = picked[a][:, tokens]
+            if a < 2:
+                lhsT_scale = picked_planes[PLANE[a] : P, tokens]
+                rhs = codes[c, a].bitcast(FP8X4)
+                rhs_scale = scales[c, a]
+            else:
+                lhsT_scale = picked_plane2[:, tokens]
+                rhs = w4_codes[c].bitcast(FP4X4)
+                rhs_scale = w4_plane[:, columns(c)]
+            nc.tensor.matmul_mx(
+                out=acc,
+                lhsT=lhsT.bitcast(FP8X4),
+                lhsT_scale=lhsT_scale,
+                rhs=rhs,
+                rhs_scale=rhs_scale,
+                start=start,
+                stop=stop,
+            )
+
+        def open_pair(c, u):
+            sums[c, u] = psum.tile([P, 2, CHUNK], F32, name=f"sum{c}{u}", tag="acc")
+
+        def pair_pass(c, u, a, start, stop):
+            for i in range(2):
+                matmul(sums[c, u][:, i, :], 2 * u + i, c, a, start and i == 0, stop and i == 1)
+
+        def finish_pair(c, u, z=None):
+            if z is None:
+                z = zpool.tile([P, 2, CHUNK], F32, name="z", align_bytes=256)
+            row = bias_held[:] if c == 2 and u < HELD else bias[:, columns(c)]
+            nc.vector.tensor_tensor(out=z[:], in0=sums[c, u][:], in1=row.unsqueeze(1).to_broadcast([P, 2, CHUNK]), op=ADD)
+            y = ypool.tile([P, 2, CHUNK], F32, name="y", align_bytes=256)
+            nc.scalar.activation(y[:], z[:], SILU)
+            dst = out[2 * u * P : 2 * (u + 1) * P, columns(c)].rearrange("(i p) n -> p i n", i=2)
+            nc.sync.dma_start(out=dst, in_=y[:])
+
+        def finish_tile(acc, t, c):
+            z = zpool.tile([P, CHUNK], F32, name="z", align_bytes=256)
+            nc.vector.tensor_tensor(out=z[:], in0=acc[:], in1=bias[:, columns(c)], op=ADD)
+            y = ypool.tile([P, CHUNK], F32, name="y", align_bytes=256)
+            nc.scalar.activation(y[:], z[:], SILU)
+            nc.sync.dma_start(out=out[t * P : (t + 1) * P, columns(c)], in_=y[:])
+
+        def load_w4_scales(queue, r):
+            queue.dma_start(out=w4_plane[r:P:32, :].bitcast(I32), in_=w4_scales[0, r:16:4, :].bitcast(I32))
+
+        table0 = kept([P, T], I32, "table0", tag="slot_table")
+        load_table(table0, 0)
+        nc.sync.dma_start(offsets[:], offs)
+        load_w4_scales(nc.gpsimd, 0)
+        nc.gpsimd.affine_select(
+            out=ident[:],
+            in_=zeros[:],
+            compare_op=mybir.AluOpType.not_equal,
+            fill=1.0,
+            base=0,
+            pattern=[[-1, P]],
+            channel_multiplier=1,
+        )
+        for q in range(4):
+            src = tab[:, (512 + 4 * q) * T : (516 + 4 * q) * T].rearrange("a (r t) -> a r t", r=4)
+            row0 = 32 * q + PLANE[0]
+            nc.gpsimd.dma_start(out=planes[row0 : row0 + 12, :].bitcast(I32), in_=src.bitcast(I32))
+
+        raw00 = placed(40 * KB, [P, 4, CHUNK], F32, "raw00")
+        load_w8(raw00[:], 0, columns(0))
+        nc.sync.dma_start(out=bias_cols[:], in_=b.rearrange("(p c) -> p c", c=8))
+        bias_held = kept([P, CHUNK], F32, "bias_held", tag="slot_held")
+        for u in range(2):
+            spread = psum.tile([P, 4, P], F32, name="spread", tag="acc")
+            for c in range(4):
+                col = bias_cols[:, 4 * u + c : 4 * u + c + 1].to_broadcast([P, P])
+                nc.tensor.transpose(spread[:, c, :], col, ident[:])
+            dst = bias[:].rearrange("q (p c) -> q p c", c=8)[:, :, 4 * u : 4 * u + 4]
+            nc.scalar.copy(dst, spread[:].rearrange("q c p -> q p c"))
+            dst = bias_held[:].rearrange("q (p c) -> q p c", c=8)[:, :, 4 * u : 4 * u + 4]
+            nc.scalar.copy(dst, spread[:, :, 64:96].rearrange("q c p -> q p c"))
+
+        table2 = placed(KB, [P, T], I32, "table2")
+        load_table(table2, 2)
+        load_w4(kept([P, 2 * CHUNK], U8, "w4_first"), 0, 1)
+        for r in range(1, 4):
+            load_w4_scales(nc.sync, r)
+
+        picked[0] = kept([P, S], U32, "picked0")
+        gather(picked[0][:], table0, 0, S)
+        table1 = kept([P, T], I32, "table1", tag="slot_table")
+        load_table(table1, 1)
+        nc.vector.tensor_copy(picked_planes[:], planes[:].indirect(offsets[:]))
+        for r in range(4):
+            nc.scalar.dma_start(
+                out=picked_plane2[r:P:32, :].bitcast(I32),
+                in_=picked_planes[PLANE[2] + r : P : 32, :].bitcast(I32),
+            )
+        grouped00 = placed(21 * KB, [P, CHUNK, 4], BF16, "grouped00")
+        interleave_on_scalar(grouped00[:], raw00[:])
+        quantize(0, (0,), grouped00[:].rearrange("p w j -> p (w j)"), words=placed(44 * KB, [P, CHUNK], U32, "codes00"))
+        raw01 = placed(40 * KB, [P, 4, CHUNK], F32, "raw01")
+        load_w8(raw01[:], 1, columns(0))
+        load_w4(placed(21 * KB + 512, [P, 2 * CHUNK], U8, "w4_second"), 1, 1)
+        raw10 = placed(17 * KB + 512, [P, 4, CHUNK], F32, "raw10")
+        load_w8(raw10[:], 0, columns(1))
+        raw11 = placed(22 * KB, [P, 4, CHUNK], F32, "raw11")
+        load_w8(raw11[:], 1, columns(1))
+
         for u in range(PAIRS):
-            pair(first[u], u, 0, 1, False, True)
+            open_pair(0, u)
+        for u in range(PAIRS):
+            pair_pass(0, u, 0, True, False)
+        picked[2] = placed(45 * KB, [P, S], U32, "picked2")
+        gather(picked[2][:], table2, 0, S)
+        load_w4(placed(16 * KB, [P, 4 * CHUNK], U8, "w4_right"), 2, 2)
+        raw2 = [placed(4 * KB * a, [P, 4, CHUNK], F32, f"raw2{a}") for a in range(2)]
+        for a in range(2):
+            load_w8(raw2[a][:], a, columns(2))
+        raw3 = placed(8 * KB, [P, 2, 4, CHUNK], F32, "raw3")
+        for a in range(2):
+            load_w8(raw3[:, a], a, columns(3))
+        for u in range(PAIRS):
+            pair_pass(0, u, 2, False, False)
+        for u in range(BANKS - PAIRS):
+            open_pair(1, u)
+        for u in range(BANKS - PAIRS):
+            pair_pass(1, u, 2, True, False)
+        picked[1] = kept([P, 2 * SLICE], U32, "picked1")
+        gather(picked[1][:], table1, 0, 2 * SLICE)
+        grouped01 = kept([P, CHUNK, 4], BF16, "grouped01", tag="slot_late")
+        interleave_on_scalar(grouped01[:], raw01[:])
+        quantize(0, (1,), grouped01[:].rearrange("p w j -> p (w j)"))
+        picked["late"] = kept([P, S - 2 * SLICE], U32, "picked1_late", tag="slot_late")
+        gather(picked["late"][:], table1, 2 * SLICE, S)
+        grouped10 = kept([P, CHUNK, 4], BF16, "grouped10", tag="slot_first")
+        interleave_on_scalar(grouped10[:], raw10[:])
+        quantize(1, (0,), grouped10[:].rearrange("p w j -> p (w j)"))
+        grouped11 = placed(30 * KB, [P, CHUNK, 4], BF16, "grouped11")
+        interleave_on_scalar(grouped11[:], raw11[:])
+        quantize(1, (1,), grouped11[:].rearrange("p w j -> p (w j)"))
+
+        grouped2 = placed(34 * KB, [P, 2, CHUNK, 4], BF16, "grouped2")
+        interleave_on_scalar(grouped2[:, 0], raw2[0][:])
+        for u in range(PAIRS):
+            pair_pass(0, u, 1, False, True)
             if u == 0:
-                z = slot("slot_z", [P, 2, NQ], F32, "z0")
+                finish_pair(0, u, kept([P, 2, CHUNK], F32, "z0", tag="slot_first"))
             elif u == 1:
-                z = placed(31 * KB, [P, 2, NQ], F32, "z1")
+                finish_pair(0, u, placed(31 * KB, [P, 2, CHUNK], F32, "z1"))
             else:
-                z = zpool.tile([P, 2, NQ], F32, name="z", align_bytes=256)
-            pair_out(first[u], u, 0, z)
+                finish_pair(0, u)
+            if u == 3:
+                nc.vector.tensor_copy(grouped2[:, 1], raw2[1][:].rearrange("p j w -> p w j"))
+
         for u in range(PAIRS):
-            if u < 2:
-                acc = second[u]
-            else:
-                acc = psum.tile([P, 2, NQ], F32, name="acc", tag="acc")
-                pair(acc, u, 1, 2, True, False)
-            pair(acc, u, 1, 0, False, False)
-            pair(acc, u, 1, 1, False, True)
-            z = zpool.tile([P, 2, NQ], F32, name="z", align_bytes=256)
-            pair_out(acc, u, 1, z)
-        for c in (2, 3):
-            for u in range(PAIRS):
-                if c == 3 and u == PAIRS - 1:
-                    for t in (2 * u, 2 * u + 1):
-                        acc = psum.tile([P, NQ], F32, name="acc", tag="acc")
-                        for a in (2, 0, 1):
-                            mm(acc[:], t, c, a, 0, NQ, a == 2, a == 1)
-                        epilogue(acc[:], t, NQ, NH)
-                else:
-                    acc = psum.tile([P, 2, NQ], F32, name="acc", tag="acc")
-                    for a in (2, 0, 1):
-                        pair(acc, u, c, a, a == 2, a == 1)
-                    z = zpool.tile([P, 2, NQ], F32, name="z", align_bytes=256)
-                    pair_out(acc, u, c, z)
+            if u >= BANKS - PAIRS:
+                open_pair(1, u)
+                pair_pass(1, u, 2, True, False)
+            pair_pass(1, u, 0, False, False)
+            pair_pass(1, u, 1, False, True)
+            finish_pair(1, u)
+            if u == 0:
+                quantize(2, (0, 1), grouped2[:].rearrange("p a w j -> p (a w j)"))
+                grouped3 = placed(34 * KB, [P, 2, CHUNK, 4], BF16, "grouped3")
+                nc.gpsimd.tensor_scalar(grouped3[:], raw3[:].rearrange("p a j w -> p a w j"), 1.0, 0.0, MULT, ADD)
+        for u in range(EARLY):
+            open_pair(2, u)
+            pair_pass(2, u, 2, True, False)
+        for c, u in [(c, u) for c in (2, 3) for u in range(PAIRS)][:-1]:
+            if (c, u) not in sums:
+                open_pair(c, u)
+                pair_pass(c, u, 2, True, False)
+            for a in (0, 1):
+                pair_pass(c, u, a, False, a == 1)
+            finish_pair(c, u)
+            if (c, u) == (2, HELD - 1):
+                quantize(3, (0, 1), grouped3[:].rearrange("p a w j -> p (a w j)"), scales_tag="slot_held")
+        for t in (TILES - 2, TILES - 1):
+            acc = psum.tile([P, CHUNK], F32, name="acc", tag="acc")
+            for a in (2, 0, 1):
+                matmul(acc[:], t, 3, a, a == 2, a == 1)
+            finish_tile(acc, t, 3)

@@ -1,6 +1,7 @@
 from contextlib import ExitStack
 
 import concourse.mybir as mybir
+from concourse.masks import make_identity
 
 F32 = mybir.dt.float32
 BF16 = mybir.dt.bfloat16
@@ -18,11 +19,10 @@ P = 128
 O, K, M, T, S = 1024, 1536, 1024, 4096, 1536
 FLOPS = 2 * K * M * S
 CHUNK = 256
-PLANE = (4, 8, 12)
 TILES = S // P
 PAIRS = TILES // 2
 BANKS = 8
-SLICE = 512
+FIRST = 1024
 HELD = 2
 EARLY = 2
 KB = 1024
@@ -47,19 +47,14 @@ def tile_list_tabo_tm_silu_kernel(tc, tab, w8, w4_words, w4_scales, b, offs, out
             return slice(c * CHUNK, (c + 1) * CHUNK)
 
         offsets = keep.tile([P, S // 16], U16, name="offsets")
-        planes = placed(44 * KB, [P, T], U8, "planes")
+        scale_rows = kept([P, T], U8, "scale_rows")
+        picked_rows = kept([P, S], U8, "picked_rows", tag="slot_last")
+        side_by_side = kept([P, 3 * S], U8, "side_by_side")
+        picked_planes = kept([P, 3 * S], U8, "picked_planes")
         w4_plane = kept([P, M], U8, "w4_plane")
-        picked_planes = kept([P, S], U8, "picked_planes")
-        picked_plane2 = kept([P, S], U8, "picked_plane2")
         bias_cols = kept([P, 8], F32, "bias_cols")
         bias = kept([P, M], F32, "bias")
         ident = kept([P, P], F32, "ident")
-        zeros = placed(17 * KB - 256, [P, P], F32, "zeros")
-
-        nc.vector.memset(w4_plane[:].bitcast(I32), 0)
-        nc.vector.memset(zeros[:], 0.0)
-        nc.vector.memset(planes[:].bitcast(I32), 0)
-        nc.vector.memset(picked_plane2[:].bitcast(I32), 0)
 
         w4_codes = {}
         codes = {}
@@ -71,14 +66,14 @@ def tile_list_tabo_tm_silu_kernel(tc, tab, w8, w4_words, w4_scales, b, offs, out
             src = tab[a, 0 : 512 * T].rearrange("(p x) -> p x", p=P)
             nc.sync.dma_start(out=words[:], in_=src.bitcast(I32))
 
-        def load_w8(raw, a, cols):
-            src = w8[512 * a : 512 * (a + 1), cols]
+        def load_w8(raw, a, c):
+            src = w8[512 * a : 512 * (a + 1), columns(c)]
             nc.sync.dma_start(out=raw, in_=src.rearrange("(p j) w -> p j w", j=4))
 
-        def load_w4(words, c, chunks):
-            src = w4_words[0, :, 2 * CHUNK * c : 2 * CHUNK * (c + chunks)]
+        def load_w4(words, c):
+            src = w4_words[0, :, 2 * CHUNK * c : 2 * CHUNK * (c + 2)]
             nc.sync.dma_start(out=words[:].bitcast(I32), in_=src.bitcast(I32))
-            for i in range(chunks):
+            for i in range(2):
                 w4_codes[c + i] = words[:, 2 * CHUNK * i : 2 * CHUNK * (i + 1)]
 
         def gather(dst, words, lo, hi):
@@ -90,10 +85,9 @@ def tile_list_tabo_tm_silu_kernel(tc, tab, w8, w4_words, w4_scales, b, offs, out
                 raw.rearrange("p j (c i) -> p c j i", i=4),
             )
 
-        def quantize(c, passes, grouped, words=None, scales_tag=None):
+        def quantize(c, passes, grouped, scales_tag=None):
             name = f"{c}{passes[0]}"
-            if words is None:
-                words = kept([P, len(passes) * CHUNK], U32, "codes" + name)
+            words = kept([P, len(passes) * CHUNK], U32, "codes" + name)
             plane = kept([P, len(passes) * CHUNK], U8, "scales" + name, tag=scales_tag)
             nc.vector.quantize_mx(out=words[:].bitcast(FP8X4), scales=plane[:], in_=grouped)
             for i, a in enumerate(passes):
@@ -101,23 +95,20 @@ def tile_list_tabo_tm_silu_kernel(tc, tab, w8, w4_words, w4_scales, b, offs, out
                 scales[c, a] = plane[:, columns(i)]
 
         def matmul(acc, t, c, a, start, stop):
-            tokens = slice(t * P, (t + 1) * P)
-            if a == 1 and t * P >= 2 * SLICE:
-                lhsT = picked["late"][:, t * P - 2 * SLICE : (t + 1) * P - 2 * SLICE]
+            if a == 1 and t * P >= FIRST:
+                lhsT = picked["late"][:, t * P - FIRST : (t + 1) * P - FIRST]
             else:
-                lhsT = picked[a][:, tokens]
+                lhsT = picked[a][:, t * P : (t + 1) * P]
             if a < 2:
-                lhsT_scale = picked_planes[PLANE[a] : P, tokens]
                 rhs = codes[c, a].bitcast(FP8X4)
                 rhs_scale = scales[c, a]
             else:
-                lhsT_scale = picked_plane2[:, tokens]
                 rhs = w4_codes[c].bitcast(FP4X4)
                 rhs_scale = w4_plane[:, columns(c)]
             nc.tensor.matmul_mx(
                 out=acc,
                 lhsT=lhsT.bitcast(FP8X4),
-                lhsT_scale=lhsT_scale,
+                lhsT_scale=picked_planes[:, a * S + t * P : a * S + (t + 1) * P],
                 rhs=rhs,
                 rhs_scale=rhs_scale,
                 start=start,
@@ -148,30 +139,42 @@ def tile_list_tabo_tm_silu_kernel(tc, tab, w8, w4_words, w4_scales, b, offs, out
             nc.scalar.activation(y[:], z[:], SILU)
             nc.sync.dma_start(out=out[t * P : (t + 1) * P, columns(c)], in_=y[:])
 
-        def load_w4_scales(queue, r):
-            queue.dma_start(out=w4_plane[r:P:32, :].bitcast(I32), in_=w4_scales[0, r:16:4, :].bitcast(I32))
-
-        table0 = kept([P, T], I32, "table0", tag="slot_table")
-        load_table(table0, 0)
+        for a in range(3):
+            src = tab[a, 512 * T : 528 * T].rearrange("(q t) -> q t", q=16)
+            nc.sync.dma_start(out=scale_rows[32 * a + 48 : 32 * a + 64, :].bitcast(I32), in_=src.bitcast(I32))
         nc.sync.dma_start(offsets[:], offs)
-        load_w4_scales(nc.gpsimd, 0)
-        nc.gpsimd.affine_select(
-            out=ident[:],
-            in_=zeros[:],
-            compare_op=mybir.AluOpType.not_equal,
-            fill=1.0,
-            base=0,
-            pattern=[[-1, P]],
-            channel_multiplier=1,
-        )
-        for q in range(4):
-            src = tab[:, (512 + 4 * q) * T : (516 + 4 * q) * T].rearrange("a (r t) -> a r t", r=4)
-            row0 = 32 * q + PLANE[0]
-            nc.gpsimd.dma_start(out=planes[row0 : row0 + 12, :].bitcast(I32), in_=src.bitcast(I32))
+        for lo, hi in ((0, 48), (64, 80), (96, 112)):
+            nc.vector.memset(scale_rows[lo:hi, :].bitcast(I32), 0)
+        nc.gpsimd.memset(picked_planes[:].bitcast(I32), 0)
+        nc.gpsimd.memset(w4_plane[:].bitcast(I32), 0)
+        nc.gpsimd.dma_start(out=bias_cols[:], in_=b.rearrange("(p c) -> p c", c=8))
+        for r in range(4):
+            nc.gpsimd.dma_start(out=w4_plane[r:P:32, :].bitcast(I32), in_=w4_scales[0, r:16:4, :].bitcast(I32))
+        make_identity(nc, ident[:])
 
-        raw00 = placed(40 * KB, [P, 4, CHUNK], F32, "raw00")
-        load_w8(raw00[:], 0, columns(0))
-        nc.sync.dma_start(out=bias_cols[:], in_=b.rearrange("(p c) -> p c", c=8))
+        table0 = placed(0, [P, T], I32, "table0")
+        load_table(table0, 0)
+        raw00 = kept([P, 4, CHUNK], F32, "raw00")
+        load_w8(raw00[:], 0, 0)
+        load_w4(kept([P, 4 * CHUNK], U8, "w4_left"), 0)
+        table2 = placed(16 * KB, [P, T], I32, "table2")
+        load_table(table2, 2)
+
+        nc.vector.tensor_copy(picked_rows[:], scale_rows[:].indirect(offsets[:]))
+        for a in range(3):
+            nc.vector.tensor_copy(
+                side_by_side[0:32, a * S : (a + 1) * S].bitcast(I32),
+                picked_rows[32 * (a + 1) : 32 * (a + 2), :].bitcast(I32),
+            )
+        for q in range(4):
+            nc.sync.dma_start(
+                out=picked_planes[32 * q : 32 * q + 4, :].bitcast(I32),
+                in_=side_by_side[16 + 4 * q : 20 + 4 * q, :].bitcast(I32),
+            )
+
+        table1 = kept([P, T], I32, "table1", tag="slot_last")
+        load_table(table1, 1)
+
         bias_held = kept([P, CHUNK], F32, "bias_held", tag="slot_held")
         for u in range(2):
             spread = psum.tile([P, 4, P], F32, name="spread", tag="acc")
@@ -183,74 +186,60 @@ def tile_list_tabo_tm_silu_kernel(tc, tab, w8, w4_words, w4_scales, b, offs, out
             dst = bias_held[:].rearrange("q (p c) -> q p c", c=8)[:, :, 4 * u : 4 * u + 4]
             nc.scalar.copy(dst, spread[:, :, 64:96].rearrange("q c p -> q p c"))
 
-        table2 = placed(KB, [P, T], I32, "table2")
-        load_table(table2, 2)
-        load_w4(kept([P, 2 * CHUNK], U8, "w4_first"), 0, 1)
-        for r in range(1, 4):
-            load_w4_scales(nc.sync, r)
-
         picked[0] = kept([P, S], U32, "picked0")
         gather(picked[0][:], table0, 0, S)
-        table1 = kept([P, T], I32, "table1", tag="slot_table")
-        load_table(table1, 1)
-        nc.vector.tensor_copy(picked_planes[:], planes[:].indirect(offsets[:]))
-        for r in range(4):
-            nc.scalar.dma_start(
-                out=picked_plane2[r:P:32, :].bitcast(I32),
-                in_=picked_planes[PLANE[2] + r : P : 32, :].bitcast(I32),
-            )
-        grouped00 = placed(21 * KB, [P, CHUNK, 4], BF16, "grouped00")
+        grouped00 = kept([P, CHUNK, 4], BF16, "grouped00")
         interleave_on_scalar(grouped00[:], raw00[:])
-        quantize(0, (0,), grouped00[:].rearrange("p w j -> p (w j)"), words=placed(44 * KB, [P, CHUNK], U32, "codes00"))
-        raw01 = placed(40 * KB, [P, 4, CHUNK], F32, "raw01")
-        load_w8(raw01[:], 1, columns(0))
-        load_w4(placed(21 * KB + 512, [P, 2 * CHUNK], U8, "w4_second"), 1, 1)
-        raw10 = placed(17 * KB + 512, [P, 4, CHUNK], F32, "raw10")
-        load_w8(raw10[:], 0, columns(1))
-        raw11 = placed(22 * KB, [P, 4, CHUNK], F32, "raw11")
-        load_w8(raw11[:], 1, columns(1))
+        quantize(0, (0,), grouped00[:].rearrange("p w j -> p (w j)"))
+
+        raw01 = placed(0, [P, 4, CHUNK], F32, "raw01")
+        load_w8(raw01[:], 1, 0)
+        raw10 = placed(4 * KB, [P, 4, CHUNK], F32, "raw10")
+        load_w8(raw10[:], 0, 1)
+        raw11 = placed(8 * KB, [P, 4, CHUNK], F32, "raw11")
+        load_w8(raw11[:], 1, 1)
+        load_w4(placed(12 * KB, [P, 4 * CHUNK], U8, "w4_right"), 2)
 
         for u in range(PAIRS):
             open_pair(0, u)
         for u in range(PAIRS):
             pair_pass(0, u, 0, True, False)
-        picked[2] = placed(45 * KB, [P, S], U32, "picked2")
+        picked[2] = kept([P, S], U32, "picked2")
         gather(picked[2][:], table2, 0, S)
-        load_w4(placed(16 * KB, [P, 4 * CHUNK], U8, "w4_right"), 2, 2)
-        raw2 = [placed(4 * KB * a, [P, 4, CHUNK], F32, f"raw2{a}") for a in range(2)]
+        raw2 = [placed(16 * KB + 4 * KB * a, [P, 4, CHUNK], F32, f"raw2{a}") for a in range(2)]
         for a in range(2):
-            load_w8(raw2[a][:], a, columns(2))
-        raw3 = placed(8 * KB, [P, 2, 4, CHUNK], F32, "raw3")
+            load_w8(raw2[a][:], a, 2)
+        raw3 = placed(24 * KB, [P, 2, 4, CHUNK], F32, "raw3")
         for a in range(2):
-            load_w8(raw3[:, a], a, columns(3))
+            load_w8(raw3[:, a], a, 3)
         for u in range(PAIRS):
             pair_pass(0, u, 2, False, False)
         for u in range(BANKS - PAIRS):
             open_pair(1, u)
         for u in range(BANKS - PAIRS):
             pair_pass(1, u, 2, True, False)
-        picked[1] = kept([P, 2 * SLICE], U32, "picked1")
-        gather(picked[1][:], table1, 0, 2 * SLICE)
+        picked[1] = kept([P, FIRST], U32, "picked1")
+        gather(picked[1][:], table1, 0, FIRST)
         grouped01 = kept([P, CHUNK, 4], BF16, "grouped01", tag="slot_late")
         interleave_on_scalar(grouped01[:], raw01[:])
         quantize(0, (1,), grouped01[:].rearrange("p w j -> p (w j)"))
-        picked["late"] = kept([P, S - 2 * SLICE], U32, "picked1_late", tag="slot_late")
-        gather(picked["late"][:], table1, 2 * SLICE, S)
+        picked["late"] = kept([P, S - FIRST], U32, "picked1_late", tag="slot_late")
+        gather(picked["late"][:], table1, FIRST, S)
         grouped10 = kept([P, CHUNK, 4], BF16, "grouped10", tag="slot_first")
         interleave_on_scalar(grouped10[:], raw10[:])
         quantize(1, (0,), grouped10[:].rearrange("p w j -> p (w j)"))
-        grouped11 = placed(30 * KB, [P, CHUNK, 4], BF16, "grouped11")
+        grouped11 = kept([P, CHUNK, 4], BF16, "grouped11", tag="slot_second")
         interleave_on_scalar(grouped11[:], raw11[:])
         quantize(1, (1,), grouped11[:].rearrange("p w j -> p (w j)"))
 
-        grouped2 = placed(34 * KB, [P, 2, CHUNK, 4], BF16, "grouped2")
+        grouped2 = kept([P, 2, CHUNK, 4], BF16, "grouped2", tag="slot_right")
         interleave_on_scalar(grouped2[:, 0], raw2[0][:])
         for u in range(PAIRS):
             pair_pass(0, u, 1, False, True)
             if u == 0:
                 finish_pair(0, u, kept([P, 2, CHUNK], F32, "z0", tag="slot_first"))
             elif u == 1:
-                finish_pair(0, u, placed(31 * KB, [P, 2, CHUNK], F32, "z1"))
+                finish_pair(0, u, kept([P, 2, CHUNK], F32, "z1", tag="slot_second"))
             else:
                 finish_pair(0, u)
             if u == 3:
@@ -265,7 +254,7 @@ def tile_list_tabo_tm_silu_kernel(tc, tab, w8, w4_words, w4_scales, b, offs, out
             finish_pair(1, u)
             if u == 0:
                 quantize(2, (0, 1), grouped2[:].rearrange("p a w j -> p (a w j)"))
-                grouped3 = placed(34 * KB, [P, 2, CHUNK, 4], BF16, "grouped3")
+                grouped3 = kept([P, 2, CHUNK, 4], BF16, "grouped3", tag="slot_right")
                 nc.gpsimd.tensor_scalar(grouped3[:], raw3[:].rearrange("p a j w -> p a w j"), 1.0, 0.0, MULT, ADD)
         for u in range(EARLY):
             open_pair(2, u)

@@ -1,7 +1,6 @@
 from contextlib import ExitStack
 
 import concourse.mybir as mybir
-from concourse.masks import make_identity
 
 F32 = mybir.dt.float32
 BF16 = mybir.dt.bfloat16
@@ -47,10 +46,9 @@ def tile_list_tabo_tm_silu_kernel(tc, tab, w8, w4_words, w4_scales, b, offs, out
             return slice(c * CHUNK, (c + 1) * CHUNK)
 
         offsets = keep.tile([P, S // 16], U16, name="offsets")
-        scale_rows = kept([P, T], U8, "scale_rows")
-        picked_rows = kept([P, S], U8, "picked_rows", tag="slot_last")
-        side_by_side = kept([P, 3 * S], U8, "side_by_side")
-        picked_planes = kept([P, 3 * S], U8, "picked_planes")
+        scale_rows = kept([P, T], U8, "scale_rows", tag="slot_last")
+        picked_rows = kept([P, S], U8, "picked_rows")
+        planes_early = kept([P, S], U8, "planes_early")
         w4_plane = kept([P, M], U8, "w4_plane")
         bias_cols = kept([P, 8], F32, "bias_cols")
         bias = kept([P, M], F32, "bias")
@@ -105,10 +103,12 @@ def tile_list_tabo_tm_silu_kernel(tc, tab, w8, w4_words, w4_scales, b, offs, out
             else:
                 rhs = w4_codes[c].bitcast(FP4X4)
                 rhs_scale = w4_plane[:, columns(c)]
+            tokens = slice(t * P, (t + 1) * P)
+            lhsT_scale = (planes_early[4:P, tokens], planes_late[:, tokens], planes_early[:, tokens])[a]
             nc.tensor.matmul_mx(
                 out=acc,
                 lhsT=lhsT.bitcast(FP8X4),
-                lhsT_scale=picked_planes[:, a * S + t * P : a * S + (t + 1) * P],
+                lhsT_scale=lhsT_scale,
                 rhs=rhs,
                 rhs_scale=rhs_scale,
                 start=start,
@@ -139,39 +139,47 @@ def tile_list_tabo_tm_silu_kernel(tc, tab, w8, w4_words, w4_scales, b, offs, out
             nc.scalar.activation(y[:], z[:], SILU)
             nc.sync.dma_start(out=out[t * P : (t + 1) * P, columns(c)], in_=y[:])
 
-        for a in range(3):
+        def load_scale_rows(a, first):
             src = tab[a, 512 * T : 528 * T].rearrange("(q t) -> q t", q=16)
-            nc.sync.dma_start(out=scale_rows[32 * a + 48 : 32 * a + 64, :].bitcast(I32), in_=src.bitcast(I32))
-        nc.sync.dma_start(offsets[:], offs)
-        for lo, hi in ((0, 48), (64, 80), (96, 112)):
-            nc.vector.memset(scale_rows[lo:hi, :].bitcast(I32), 0)
-        nc.gpsimd.memset(picked_planes[:].bitcast(I32), 0)
-        nc.gpsimd.memset(w4_plane[:].bitcast(I32), 0)
-        nc.gpsimd.dma_start(out=bias_cols[:], in_=b.rearrange("(p c) -> p c", c=8))
-        for r in range(4):
-            nc.gpsimd.dma_start(out=w4_plane[r:P:32, :].bitcast(I32), in_=w4_scales[0, r:16:4, :].bitcast(I32))
-        make_identity(nc, ident[:])
+            nc.sync.dma_start(out=scale_rows[first : first + 32 : 2, :].bitcast(I32), in_=src.bitcast(I32))
 
-        table0 = placed(0, [P, T], I32, "table0")
-        load_table(table0, 0)
+        def carry(planes, first):
+            for r in range(4):
+                rows = picked_rows[first + 2 * r : first + 2 * r + 32, :]
+                nc.sync.dma_start(out=planes[r:P:4, :].bitcast(I32), in_=rows.bitcast(I32))
+
+        load_scale_rows(2, 0)
+        load_scale_rows(0, 1)
+        nc.sync.dma_start(offsets[:], offs)
         raw00 = kept([P, 4, CHUNK], F32, "raw00")
         load_w8(raw00[:], 0, 0)
         load_w4(kept([P, 4 * CHUNK], U8, "w4_left"), 0)
+        nc.sync.dma_start(out=bias_cols[:], in_=b.rearrange("(p c) -> p c", c=8))
+        nc.vector.memset(scale_rows[64:P, :].bitcast(I32), 0)
+        load_scale_rows(1, 64)
+        zeros = placed(16 * KB - 256, [P, P], F32, "zeros")
+        nc.vector.memset(zeros[:], 0.0)
+        nc.vector.memset(scale_rows[32:64, :].bitcast(I32), 0)
+        nc.vector.memset(w4_plane[:].bitcast(I32), 0)
+        nc.gpsimd.affine_select(
+            out=ident[:],
+            in_=zeros[:],
+            compare_op=mybir.AluOpType.not_equal,
+            fill=1.0,
+            base=0,
+            pattern=[[-1, P]],
+            channel_multiplier=1,
+        )
+        for r in range(4):
+            nc.gpsimd.dma_start(out=w4_plane[r:P:32, :].bitcast(I32), in_=w4_scales[0, r:16:4, :].bitcast(I32))
+
+        table0 = placed(0, [P, T], I32, "table0")
+        load_table(table0, 0)
         table2 = placed(16 * KB, [P, T], I32, "table2")
         load_table(table2, 2)
 
         nc.vector.tensor_copy(picked_rows[:], scale_rows[:].indirect(offsets[:]))
-        for a in range(3):
-            nc.vector.tensor_copy(
-                side_by_side[0:32, a * S : (a + 1) * S].bitcast(I32),
-                picked_rows[32 * (a + 1) : 32 * (a + 2), :].bitcast(I32),
-            )
-        for q in range(4):
-            nc.sync.dma_start(
-                out=picked_planes[32 * q : 32 * q + 4, :].bitcast(I32),
-                in_=side_by_side[16 + 4 * q : 20 + 4 * q, :].bitcast(I32),
-            )
-
+        carry(planes_early, 0)
         table1 = kept([P, T], I32, "table1", tag="slot_last")
         load_table(table1, 1)
 
@@ -194,11 +202,13 @@ def tile_list_tabo_tm_silu_kernel(tc, tab, w8, w4_words, w4_scales, b, offs, out
 
         raw01 = placed(0, [P, 4, CHUNK], F32, "raw01")
         load_w8(raw01[:], 1, 0)
+        planes_late = placed(12 * KB, [P, S], U8, "planes_late")
+        carry(planes_late, 64)
         raw10 = placed(4 * KB, [P, 4, CHUNK], F32, "raw10")
         load_w8(raw10[:], 0, 1)
         raw11 = placed(8 * KB, [P, 4, CHUNK], F32, "raw11")
         load_w8(raw11[:], 1, 1)
-        load_w4(placed(12 * KB, [P, 4 * CHUNK], U8, "w4_right"), 2)
+        load_w4(placed(14 * KB, [P, 4 * CHUNK], U8, "w4_right"), 2)
 
         for u in range(PAIRS):
             open_pair(0, u)

@@ -1,6 +1,7 @@
 from contextlib import ExitStack
 
 import concourse.mybir as mybir
+from concourse.masks import make_identity
 
 F32 = mybir.dt.float32
 BF16 = mybir.dt.bfloat16
@@ -139,47 +140,33 @@ def tile_list_tabo_tm_silu_kernel(tc, tab, w8, w4_words, w4_scales, b, offs, out
             nc.scalar.activation(y[:], z[:], SILU)
             nc.sync.dma_start(out=out[t * P : (t + 1) * P, columns(c)], in_=y[:])
 
-        def load_scale_rows(a, first):
+        def load_scale_rows(a, rows):
             src = tab[a, 512 * T : 528 * T].rearrange("(q t) -> q t", q=16)
-            nc.sync.dma_start(out=scale_rows[first : first + 32 : 2, :].bitcast(I32), in_=src.bitcast(I32))
+            nc.sync.dma_start(out=scale_rows[rows, :].bitcast(I32), in_=src.bitcast(I32))
 
-        def carry(planes, first):
-            for r in range(4):
-                rows = picked_rows[first + 2 * r : first + 2 * r + 32, :]
-                nc.sync.dma_start(out=planes[r:P:4, :].bitcast(I32), in_=rows.bitcast(I32))
-
-        load_scale_rows(2, 0)
-        load_scale_rows(0, 1)
+        load_scale_rows(2, slice(0, 32, 2))
+        load_scale_rows(1, slice(112, P))
+        load_scale_rows(0, slice(1, 32, 2))
         nc.sync.dma_start(offsets[:], offs)
+        nc.sync.dma_start(out=bias_cols[:], in_=b.rearrange("(p c) -> p c", c=8))
+        table0 = placed(0, [P, T], I32, "table0")
+        load_table(table0, 0)
         raw00 = kept([P, 4, CHUNK], F32, "raw00")
         load_w8(raw00[:], 0, 0)
         load_w4(kept([P, 4 * CHUNK], U8, "w4_left"), 0)
-        nc.sync.dma_start(out=bias_cols[:], in_=b.rearrange("(p c) -> p c", c=8))
-        nc.vector.memset(scale_rows[64:P, :].bitcast(I32), 0)
-        load_scale_rows(1, 64)
-        zeros = placed(16 * KB - 256, [P, P], F32, "zeros")
-        nc.vector.memset(zeros[:], 0.0)
-        nc.vector.memset(scale_rows[32:64, :].bitcast(I32), 0)
         nc.vector.memset(w4_plane[:].bitcast(I32), 0)
-        nc.gpsimd.affine_select(
-            out=ident[:],
-            in_=zeros[:],
-            compare_op=mybir.AluOpType.not_equal,
-            fill=1.0,
-            base=0,
-            pattern=[[-1, P]],
-            channel_multiplier=1,
-        )
         for r in range(4):
-            nc.gpsimd.dma_start(out=w4_plane[r:P:32, :].bitcast(I32), in_=w4_scales[0, r:16:4, :].bitcast(I32))
-
-        table0 = placed(0, [P, T], I32, "table0")
-        load_table(table0, 0)
+            nc.sync.dma_start(out=w4_plane[r:P:32, :].bitcast(I32), in_=w4_scales[0, r:16:4, :].bitcast(I32))
+        make_identity(nc, ident[:])
+        nc.vector.memset(scale_rows[32:64, :].bitcast(I32), 0)
+        nc.vector.memset(scale_rows[64:112, :].bitcast(I32), 0)
         table2 = placed(16 * KB, [P, T], I32, "table2")
         load_table(table2, 2)
 
         nc.vector.tensor_copy(picked_rows[:], scale_rows[:].indirect(offsets[:]))
-        carry(planes_early, 0)
+        for r in range(4):
+            rows = picked_rows[2 * r : 2 * r + 32, :]
+            nc.sync.dma_start(out=planes_early[r:P:4, :].bitcast(I32), in_=rows.bitcast(I32))
         table1 = kept([P, T], I32, "table1", tag="slot_last")
         load_table(table1, 1)
 
@@ -202,24 +189,26 @@ def tile_list_tabo_tm_silu_kernel(tc, tab, w8, w4_words, w4_scales, b, offs, out
 
         raw01 = placed(0, [P, 4, CHUNK], F32, "raw01")
         load_w8(raw01[:], 1, 0)
-        planes_late = placed(12 * KB, [P, S], U8, "planes_late")
-        carry(planes_late, 64)
-        raw10 = placed(4 * KB, [P, 4, CHUNK], F32, "raw10")
-        load_w8(raw10[:], 0, 1)
-        raw11 = placed(8 * KB, [P, 4, CHUNK], F32, "raw11")
-        load_w8(raw11[:], 1, 1)
-        load_w4(placed(14 * KB, [P, 4 * CHUNK], U8, "w4_right"), 2)
-
+        planes_late = placed(4 * KB, [P, S], U8, "planes_late")
+        nc.vector.memset(planes_late[:].bitcast(I32), 0)
+        for r in range(4):
+            rows = picked_rows[112 + r : P : 4, :]
+            nc.sync.dma_start(out=planes_late[r:P:32, :].bitcast(I32), in_=rows.bitcast(I32))
         for u in range(PAIRS):
             open_pair(0, u)
         for u in range(PAIRS):
             pair_pass(0, u, 0, True, False)
         picked[2] = kept([P, S], U32, "picked2")
         gather(picked[2][:], table2, 0, S)
-        raw2 = [placed(16 * KB + 4 * KB * a, [P, 4, CHUNK], F32, f"raw2{a}") for a in range(2)]
+        raw10 = placed(12 * KB + 256, [P, 4, CHUNK], F32, "raw10")
+        load_w8(raw10[:], 0, 1)
+        raw11 = placed(16 * KB + 256, [P, 4, CHUNK], F32, "raw11")
+        load_w8(raw11[:], 1, 1)
+        load_w4(placed(20 * KB + 256, [P, 4 * CHUNK], U8, "w4_right"), 2)
+        raw2 = [placed(21 * KB + 256 + 4 * KB * a, [P, 4, CHUNK], F32, f"raw2{a}") for a in range(2)]
         for a in range(2):
             load_w8(raw2[a][:], a, 2)
-        raw3 = placed(24 * KB, [P, 2, 4, CHUNK], F32, "raw3")
+        raw3 = placed(29 * KB + 256, [P, 2, 4, CHUNK], F32, "raw3")
         for a in range(2):
             load_w8(raw3[:, a], a, 3)
         for u in range(PAIRS):

@@ -69,10 +69,10 @@ def tile_list_tabo_tm_silu_kernel(tc, tab, w8, w4_words, w4_scales, b, offs, out
             src = w8[512 * a : 512 * (a + 1), columns(c)]
             nc.sync.dma_start(out=raw, in_=src.rearrange("(p j) w -> p j w", j=4))
 
-        def load_w4(words, c):
-            src = w4_words[0, :, 2 * CHUNK * c : 2 * CHUNK * (c + 2)]
+        def load_w4(words, c, chunks):
+            src = w4_words[0, :, 2 * CHUNK * c : 2 * CHUNK * (c + chunks)]
             nc.sync.dma_start(out=words[:].bitcast(I32), in_=src.bitcast(I32))
-            for i in range(2):
+            for i in range(chunks):
                 w4_codes[c + i] = words[:, 2 * CHUNK * i : 2 * CHUNK * (i + 1)]
 
         def gather(dst, words, lo, hi):
@@ -153,10 +153,10 @@ def tile_list_tabo_tm_silu_kernel(tc, tab, w8, w4_words, w4_scales, b, offs, out
         load_table(table0, 0)
         raw00 = kept([P, 4, CHUNK], F32, "raw00")
         load_w8(raw00[:], 0, 0)
-        load_w4(kept([P, 4 * CHUNK], U8, "w4_left"), 0)
+        load_w4(kept([P, 2 * CHUNK], U8, "w4_first"), 0, 1)
         nc.vector.memset(w4_plane[:].bitcast(I32), 0)
-        for r in range(4):
-            nc.sync.dma_start(out=w4_plane[r:P:32, :].bitcast(I32), in_=w4_scales[0, r:16:4, :].bitcast(I32))
+        w4_rows = kept([P, 4, M], U8, "w4_rows")
+        nc.sync.dma_start(out=w4_rows[0:4].bitcast(I32), in_=w4_scales[0].rearrange("(q r) n -> r q n", r=4).bitcast(I32))
         make_identity(nc, ident[:])
         nc.vector.memset(scale_rows[32:64, :].bitcast(I32), 0)
         nc.vector.memset(scale_rows[64:112, :].bitcast(I32), 0)
@@ -166,7 +166,7 @@ def tile_list_tabo_tm_silu_kernel(tc, tab, w8, w4_words, w4_scales, b, offs, out
         nc.vector.tensor_copy(picked_rows[:], scale_rows[:].indirect(offsets[:]))
         for r in range(4):
             rows = picked_rows[2 * r : 2 * r + 32, :]
-            nc.sync.dma_start(out=planes_early[r:P:4, :].bitcast(I32), in_=rows.bitcast(I32))
+            nc.scalar.dma_start(out=planes_early[r:P:4, :].bitcast(I32), in_=rows.bitcast(I32))
         table1 = kept([P, T], I32, "table1", tag="slot_last")
         load_table(table1, 1)
 
@@ -187,13 +187,16 @@ def tile_list_tabo_tm_silu_kernel(tc, tab, w8, w4_words, w4_scales, b, offs, out
         interleave_on_scalar(grouped00[:], raw00[:])
         quantize(0, (0,), grouped00[:].rearrange("p w j -> p (w j)"))
 
+        for q in range(4):
+            nc.vector.tensor_copy(w4_plane[32 * q : 32 * q + 4, :].bitcast(I32), w4_rows[0:4, q, :].bitcast(I32))
         raw01 = placed(0, [P, 4, CHUNK], F32, "raw01")
         load_w8(raw01[:], 1, 0)
+        load_w4(placed(6 * KB, [P, 2 * CHUNK], U8, "w4_second"), 1, 1)
         planes_late = placed(4 * KB, [P, S], U8, "planes_late")
         nc.vector.memset(planes_late[:].bitcast(I32), 0)
         for r in range(4):
             rows = picked_rows[112 + r : P : 4, :]
-            nc.sync.dma_start(out=planes_late[r:P:32, :].bitcast(I32), in_=rows.bitcast(I32))
+            nc.scalar.dma_start(out=planes_late[r:P:32, :].bitcast(I32), in_=rows.bitcast(I32))
         for u in range(PAIRS):
             open_pair(0, u)
         for u in range(PAIRS):
@@ -204,7 +207,7 @@ def tile_list_tabo_tm_silu_kernel(tc, tab, w8, w4_words, w4_scales, b, offs, out
         load_w8(raw10[:], 0, 1)
         raw11 = placed(16 * KB + 256, [P, 4, CHUNK], F32, "raw11")
         load_w8(raw11[:], 1, 1)
-        load_w4(placed(20 * KB + 256, [P, 4 * CHUNK], U8, "w4_right"), 2)
+        load_w4(placed(20 * KB + 256, [P, 4 * CHUNK], U8, "w4_right"), 2, 2)
         raw2 = [placed(21 * KB + 256 + 4 * KB * a, [P, 4, CHUNK], F32, f"raw2{a}") for a in range(2)]
         for a in range(2):
             load_w8(raw2[a][:], a, 2)

from contextlib import ExitStack

import concourse.mybir as mybir
from concourse.masks import make_identity

F32 = mybir.dt.float32
BF16 = mybir.dt.bfloat16
I32 = mybir.dt.int32
U32 = mybir.dt.uint32
U16 = mybir.dt.uint16
U8 = mybir.dt.uint8
FP8X4 = mybir.dt.float8_e4m3fn_x4
FP4X4 = mybir.dt.float4_e2m1fn_x4
ADD = mybir.AluOpType.add
MULT = mybir.AluOpType.mult
SILU = mybir.ActivationFunctionType.Silu

P = 128
O, K, M, T, S = 1024, 1536, 1024, 4096, 1536
FLOPS = 2 * K * M * S
CHUNK = 256
TILES = S // P
PAIRS = TILES // 2
BANKS = 8
FIRST = 1024
HELD = 2
EARLY = 2
KB = 1024


def tile_list_tabo_tm_silu_kernel(tc, tab, w8, w4_words, w4_scales, b, offs, out):
    nc = tc.nc
    with ExitStack() as ctx:
        keep = ctx.enter_context(tc.tile_pool(name="keep", bufs=1))
        stage = ctx.enter_context(tc.tile_pool(name="stage", bufs=1))
        zpool = ctx.enter_context(tc.tile_pool(name="zpool", bufs=10))
        ypool = ctx.enter_context(tc.tile_pool(name="ypool", bufs=25))
        psum = ctx.enter_context(tc.psum_pool(name="psum", bufs=BANKS))

        def kept(shape, dtype, name, tag=None):
            return keep.tile(shape, dtype, name=name, tag=tag or name, align_bytes=256)

        def placed(offset, shape, dtype, name):
            return stage.tile(shape, dtype, name=name, align_bytes=256, offset=offset)

        def columns(c):
            return slice(c * CHUNK, (c + 1) * CHUNK)

        offsets = keep.tile([P, S // 16], U16, name="offsets")
        scale_rows = kept([P, T], U8, "scale_rows", tag="slot_last")
        picked_rows = kept([P, S], U8, "picked_rows")
        planes_early = kept([P, S], U8, "planes_early")
        w4_plane = kept([P, M], U8, "w4_plane")
        bias_cols = kept([P, 8], F32, "bias_cols")
        bias = kept([P, M], F32, "bias")
        ident = kept([P, P], F32, "ident")

        w4_codes = {}
        codes = {}
        scales = {}
        picked = {}
        sums = {}

        def load_table(words, a):
            src = tab[a, 0 : 512 * T].rearrange("(p x) -> p x", p=P)
            nc.sync.dma_start(out=words[:], in_=src.bitcast(I32))

        def load_w8(raw, a, c):
            src = w8[512 * a : 512 * (a + 1), columns(c)]
            nc.sync.dma_start(out=raw, in_=src.rearrange("(p j) w -> p j w", j=4))

        def load_w4(words, c, chunks):
            src = w4_words[0, :, 2 * CHUNK * c : 2 * CHUNK * (c + chunks)]
            nc.sync.dma_start(out=words[:].bitcast(I32), in_=src.bitcast(I32))
            for i in range(chunks):
                w4_codes[c + i] = words[:, 2 * CHUNK * i : 2 * CHUNK * (i + 1)]

        def gather(dst, words, lo, hi):
            nc.vector.tensor_copy(dst, words[:].bitcast(U32).indirect(offsets[:, lo // 16 : hi // 16]))

        def interleave_on_scalar(grouped, raw):
            nc.scalar.copy(
                grouped.rearrange("p (c i) j -> p c j i", i=4),
                raw.rearrange("p j (c i) -> p c j i", i=4),
            )

        def quantize(c, passes, grouped, scales_tag=None):
            name = f"{c}{passes[0]}"
            words = kept([P, len(passes) * CHUNK], U32, "codes" + name)
            plane = kept([P, len(passes) * CHUNK], U8, "scales" + name, tag=scales_tag)
            nc.vector.quantize_mx(out=words[:].bitcast(FP8X4), scales=plane[:], in_=grouped)
            for i, a in enumerate(passes):
                codes[c, a] = words[:, columns(i)]
                scales[c, a] = plane[:, columns(i)]

        def matmul(acc, t, c, a, start, stop):
            if a == 1 and t * P >= FIRST:
                lhsT = picked["late"][:, t * P - FIRST : (t + 1) * P - FIRST]
            else:
                lhsT = picked[a][:, t * P : (t + 1) * P]
            if a < 2:
                rhs = codes[c, a].bitcast(FP8X4)
                rhs_scale = scales[c, a]
            else:
                rhs = w4_codes[c].bitcast(FP4X4)
                rhs_scale = w4_plane[:, columns(c)]
            tokens = slice(t * P, (t + 1) * P)
            lhsT_scale = (planes_early[4:P, tokens], planes_late[:, tokens], planes_early[:, tokens])[a]
            nc.tensor.matmul_mx(
                out=acc,
                lhsT=lhsT.bitcast(FP8X4),
                lhsT_scale=lhsT_scale,
                rhs=rhs,
                rhs_scale=rhs_scale,
                start=start,
                stop=stop,
            )

        def open_pair(c, u):
            sums[c, u] = psum.tile([P, 2, CHUNK], F32, name=f"sum{c}{u}", tag="acc")

        def pair_pass(c, u, a, start, stop):
            for i in range(2):
                matmul(sums[c, u][:, i, :], 2 * u + i, c, a, start and i == 0, stop and i == 1)

        def finish_pair(c, u, z=None):
            if z is None:
                z = zpool.tile([P, 2, CHUNK], F32, name="z", align_bytes=256)
            row = bias_held[:] if c == 2 and u < HELD else bias[:, columns(c)]
            nc.vector.tensor_tensor(out=z[:], in0=sums[c, u][:], in1=row.unsqueeze(1).to_broadcast([P, 2, CHUNK]), op=ADD)
            y = ypool.tile([P, 2, CHUNK], F32, name="y", align_bytes=256)
            nc.scalar.activation(y[:], z[:], SILU)
            dst = out[2 * u * P : 2 * (u + 1) * P, columns(c)].rearrange("(i p) n -> p i n", i=2)
            nc.sync.dma_start(out=dst, in_=y[:])

        def finish_tile(acc, t, c):
            z = zpool.tile([P, CHUNK], F32, name="z", align_bytes=256)
            nc.vector.tensor_tensor(out=z[:], in0=acc[:], in1=bias[:, columns(c)], op=ADD)
            y = ypool.tile([P, CHUNK], F32, name="y", align_bytes=256)
            nc.scalar.activation(y[:], z[:], SILU)
            nc.sync.dma_start(out=out[t * P : (t + 1) * P, columns(c)], in_=y[:])

        def load_scale_rows(a, rows):
            src = tab[a, 512 * T : 528 * T].rearrange("(q t) -> q t", q=16)
            nc.sync.dma_start(out=scale_rows[rows, :].bitcast(I32), in_=src.bitcast(I32))

        load_scale_rows(2, slice(0, 32, 2))
        load_scale_rows(1, slice(112, P))
        load_scale_rows(0, slice(1, 32, 2))
        nc.sync.dma_start(offsets[:], offs)
        nc.sync.dma_start(out=bias_cols[:], in_=b.rearrange("(p c) -> p c", c=8))
        table0 = placed(0, [P, T], I32, "table0")
        load_table(table0, 0)
        raw00 = kept([P, 4, CHUNK], F32, "raw00")
        load_w8(raw00[:], 0, 0)
        load_w4(kept([P, 2 * CHUNK], U8, "w4_first"), 0, 1)
        nc.vector.memset(w4_plane[:].bitcast(I32), 0)
        w4_rows = kept([P, 4, M], U8, "w4_rows")
        nc.sync.dma_start(out=w4_rows[0:4].bitcast(I32), in_=w4_scales[0].rearrange("(q r) n -> r q n", r=4).bitcast(I32))
        make_identity(nc, ident[:])
        nc.vector.memset(scale_rows[32:64, :].bitcast(I32), 0)
        nc.vector.memset(scale_rows[64:112, :].bitcast(I32), 0)
        table2 = placed(16 * KB, [P, T], I32, "table2")
        load_table(table2, 2)

        nc.vector.tensor_copy(picked_rows[:], scale_rows[:].indirect(offsets[:]))
        for r in range(4):
            rows = picked_rows[2 * r : 2 * r + 32, :]
            nc.scalar.dma_start(out=planes_early[r:P:4, :].bitcast(I32), in_=rows.bitcast(I32))
        table1 = kept([P, T], I32, "table1", tag="slot_last")
        load_table(table1, 1)

        bias_held = kept([P, CHUNK], F32, "bias_held", tag="slot_held")
        for u in range(2):
            spread = psum.tile([P, 4, P], F32, name="spread", tag="acc")
            for c in range(4):
                col = bias_cols[:, 4 * u + c : 4 * u + c + 1].to_broadcast([P, P])
                nc.tensor.transpose(spread[:, c, :], col, ident[:])
            dst = bias[:].rearrange("q (p c) -> q p c", c=8)[:, :, 4 * u : 4 * u + 4]
            nc.scalar.copy(dst, spread[:].rearrange("q c p -> q p c"))
            dst = bias_held[:].rearrange("q (p c) -> q p c", c=8)[:, :, 4 * u : 4 * u + 4]
            nc.scalar.copy(dst, spread[:, :, 64:96].rearrange("q c p -> q p c"))

        picked[0] = kept([P, S], U32, "picked0")
        gather(picked[0][:], table0, 0, S)
        grouped00 = kept([P, CHUNK, 4], BF16, "grouped00")
        interleave_on_scalar(grouped00[:], raw00[:])
        quantize(0, (0,), grouped00[:].rearrange("p w j -> p (w j)"))

        for q in range(4):
            nc.vector.tensor_copy(w4_plane[32 * q : 32 * q + 4, :].bitcast(I32), w4_rows[0:4, q, :].bitcast(I32))
        raw01 = placed(0, [P, 4, CHUNK], F32, "raw01")
        load_w8(raw01[:], 1, 0)
        load_w4(placed(6 * KB, [P, 2 * CHUNK], U8, "w4_second"), 1, 1)
        planes_late = placed(4 * KB, [P, S], U8, "planes_late")
        nc.vector.memset(planes_late[:].bitcast(I32), 0)
        for r in range(4):
            rows = picked_rows[112 + r : P : 4, :]
            nc.scalar.dma_start(out=planes_late[r:P:32, :].bitcast(I32), in_=rows.bitcast(I32))
        for u in range(PAIRS):
            open_pair(0, u)
        for u in range(PAIRS):
            pair_pass(0, u, 0, True, False)
        picked[2] = kept([P, S], U32, "picked2")
        gather(picked[2][:], table2, 0, S)
        raw10 = placed(12 * KB + 256, [P, 4, CHUNK], F32, "raw10")
        load_w8(raw10[:], 0, 1)
        raw11 = placed(16 * KB + 256, [P, 4, CHUNK], F32, "raw11")
        load_w8(raw11[:], 1, 1)
        load_w4(placed(20 * KB + 256, [P, 4 * CHUNK], U8, "w4_right"), 2, 2)
        raw2 = [placed(21 * KB + 256 + 4 * KB * a, [P, 4, CHUNK], F32, f"raw2{a}") for a in range(2)]
        for a in range(2):
            load_w8(raw2[a][:], a, 2)
        raw3 = placed(29 * KB + 256, [P, 2, 4, CHUNK], F32, "raw3")
        for a in range(2):
            load_w8(raw3[:, a], a, 3)
        for u in range(PAIRS):
            pair_pass(0, u, 2, False, False)
        for u in range(BANKS - PAIRS):
            open_pair(1, u)
        for u in range(BANKS - PAIRS):
            pair_pass(1, u, 2, True, False)
        picked[1] = kept([P, FIRST], U32, "picked1")
        gather(picked[1][:], table1, 0, FIRST)
        grouped01 = kept([P, CHUNK, 4], BF16, "grouped01", tag="slot_late")
        interleave_on_scalar(grouped01[:], raw01[:])
        quantize(0, (1,), grouped01[:].rearrange("p w j -> p (w j)"))
        picked["late"] = kept([P, S - FIRST], U32, "picked1_late", tag="slot_late")
        gather(picked["late"][:], table1, FIRST, S)
        grouped10 = kept([P, CHUNK, 4], BF16, "grouped10", tag="slot_first")
        interleave_on_scalar(grouped10[:], raw10[:])
        quantize(1, (0,), grouped10[:].rearrange("p w j -> p (w j)"))
        grouped11 = kept([P, CHUNK, 4], BF16, "grouped11", tag="slot_second")
        interleave_on_scalar(grouped11[:], raw11[:])
        quantize(1, (1,), grouped11[:].rearrange("p w j -> p (w j)"))

        grouped2 = kept([P, 2, CHUNK, 4], BF16, "grouped2", tag="slot_right")
        interleave_on_scalar(grouped2[:, 0], raw2[0][:])
        for u in range(PAIRS):
            pair_pass(0, u, 1, False, True)
            if u == 0:
                finish_pair(0, u, kept([P, 2, CHUNK], F32, "z0", tag="slot_first"))
            elif u == 1:
                finish_pair(0, u, kept([P, 2, CHUNK], F32, "z1", tag="slot_second"))
            else:
                finish_pair(0, u)
            if u == 3:
                nc.vector.tensor_copy(grouped2[:, 1], raw2[1][:].rearrange("p j w -> p w j"))

        for u in range(PAIRS):
            if u >= BANKS - PAIRS:
                open_pair(1, u)
                pair_pass(1, u, 2, True, False)
            pair_pass(1, u, 0, False, False)
            pair_pass(1, u, 1, False, True)
            finish_pair(1, u)
            if u == 0:
                quantize(2, (0, 1), grouped2[:].rearrange("p a w j -> p (a w j)"))
                grouped3 = kept([P, 2, CHUNK, 4], BF16, "grouped3", tag="slot_right")
                nc.gpsimd.tensor_scalar(grouped3[:], raw3[:].rearrange("p a j w -> p a w j"), 1.0, 0.0, MULT, ADD)
        for u in range(EARLY):
            open_pair(2, u)
            pair_pass(2, u, 2, True, False)
        for c, u in [(c, u) for c in (2, 3) for u in range(PAIRS)][:-1]:
            if (c, u) not in sums:
                open_pair(c, u)
                pair_pass(c, u, 2, True, False)
            for a in (0, 1):
                pair_pass(c, u, a, False, a == 1)
            finish_pair(c, u)
            if (c, u) == (2, HELD - 1):
                quantize(3, (0, 1), grouped3[:].rearrange("p a w j -> p (a w j)"), scales_tag="slot_held")
        for t in (TILES - 2, TILES - 1):
            acc = psum.tile([P, CHUNK], F32, name="acc", tag="acc")
            for a in (2, 0, 1):
                matmul(acc[:], t, 3, a, a == 2, a == 1)
            finish_tile(acc, t, 3)
